import numpy as np
import ml_dtypes


def mxq(x, axis, fmt="e4m3"):
    dtype, down = {"e4m3": (ml_dtypes.float8_e4m3fn, 7), "e5m2": (ml_dtypes.float8_e5m2, 14)}[fmt]
    v = np.moveaxis(np.asarray(x, np.float32).astype(ml_dtypes.bfloat16).astype(np.float64), axis, -1)
    blocks = v.reshape(v.shape[:-1] + (-1, 32))
    amax = np.abs(blocks).max(-1, keepdims=True)
    byte = np.maximum(np.where(amax > 0, np.frexp(amax)[1] - 1 + 127, 0) - down, 1)
    scale = np.exp2(byte - 127.0)
    codes = (blocks / scale).astype(np.float32).astype(dtype).astype(np.float64)
    return np.moveaxis((codes * scale).reshape(v.shape), -1, axis)


WIDE = False


def mx_kscale(k):
    if not WIDE:
        return np.ones(k)
    levels = np.array([10, -10, 5, -5, 0])
    if k % 512:
        return np.exp2(np.random.permutation(np.resize(levels, k // 32))).repeat(32)
    a = np.empty((k // 512, 16))
    for p in range(k // 512):
        a[p, :8] = np.random.permutation(np.resize(levels, 8))
        for g in range(8):
            far = levels[np.abs(levels - a[p, g]) >= 10]
            a[p, g + 8] = far[np.random.randint(len(far))]
    return np.exp2(a.ravel()).repeat(32)


def f64(x):
    return np.asarray(x).astype(np.float64)


def striped(idx):
    return np.tile(np.asarray(idx).reshape(-1, 16).T, (8, 1)).astype(np.uint16)


def unstriped(offs):
    return offs[:16].T.reshape(-1).astype(np.int64)


B, N, T, D, DV, NQ = 1, 512, 1024, 512, 256, 128
CAP = 2.0


def setup_inputs():
    n = np.random.standard_normal
    idx = np.sort(np.random.permutation(T)[:B * N].reshape(B, N), axis=1).reshape(-1)
    s = mx_kscale(D)[:, None]
    u = np.ones(T)
    u[idx] = mx_kscale(B * N)
    r = np.random.uniform(0.5, 2.0, T)
    k = n((D, T)) / s
    v = n((DV, T)) / (u * r)
    return {
        "qT": (n((B, D, NQ)) * s * (0.60 / np.sqrt(D))).astype(np.float32),
        "kT": k.astype(np.float32),
        "vT": v.astype(np.float32),
        "vs": np.tile(u * r, (128, 1)).astype(np.float32),
        "offs": striped(idx),
    }


def reference(qT, kT, vT, vs, offs):
    idx = unstriped(offs)
    k = f64(kT)
    v = f64(vT)
    pick = lambda x: x[:, idx].reshape(x.shape[0], B, N).transpose(1, 0, 2)
    q = f64(qT)
    score = mxq(q, 1, "e4m3").transpose(0, 2, 1) @ mxq(pick(k), 1, "e4m3")
    score = CAP * np.tanh(score / CAP)
    p = 1.0 / (1.0 + np.exp(-score))
    w = p * pick(f64(vs))[:, :1, :]
    y = mxq(w, 2, "e4m3") @ mxq(pick(v).transpose(0, 2, 1), 1, "e4m3")
    y = y / 16.0
    return y

@@ -1,0 +1,173 @@
+from contextlib import ExitStack
+
+import concourse.mybir as mybir
+from concourse.masks import make_identity
+
+N, T, D, DV, NQ = 512, 1024, 512, 256, 128
+FLOPS = 2 * NQ * N * D + 2 * NQ * N * DV
+BYTES = 4 * (D * NQ + D * T + DV * T + T + NQ * DV) + 2 * 128 * (N // 16)
+
+F32 = mybir.dt.float32
+BF16 = mybir.dt.bfloat16
+U32 = mybir.dt.uint32
+U16 = mybir.dt.uint16
+U8 = mybir.dt.uint8
+FP8X4 = mybir.dt.float8_e4m3fn_x4
+ACT = mybir.ActivationFunctionType
+ALU = mybir.AluOpType
+
+P = 128
+PACK = 4
+HALF = N // 2
+
+
+def tile_attend_x_sigmoid_cap_srt_kernel(tc, qT, kT, vT, vs, offs, out):
+    nc = tc.nc
+    with ExitStack() as ctx:
+        sb = ctx.enter_context(tc.tile_pool(name="sb", bufs=1))
+        ps = ctx.enter_context(tc.psum_pool(name="ps", bufs=1))
+
+        offsets = sb.tile([P, N // 16], U16, name="offsets")
+        nc.sync.dma_start(offsets[:], offs)
+
+        ident = sb.tile([P, P], F32, name="ident")
+        make_identity(nc, ident[:])
+
+        warm_in = sb.tile([P, 8], F32, name="warm_in")
+        warm = sb.tile([P, 8], F32, name="warm")
+        nc.vector.memset(warm_in[:], 0.0)
+        nc.scalar.activation(warm[:], warm_in[:], ACT.Tanh)
+
+        vs_pool = sb.tile([P, T], F32, name="vs_pool")
+        nc.vector.memset(vs_pool[:], 0.0)
+
+        q_raw = sb.tile([P, PACK, NQ], F32, name="q_raw")
+        nc.sync.dma_start(q_raw[:], qT[0].rearrange("(p j) n -> p j n", j=PACK))
+        k_rows = kT.rearrange("(p u e) n -> p u e n", u=2, e=2)
+        pieces = [(0, 0, 512), (0, 512, 1024), (1, 0, 512), (1, 512, 768), (1, 768, 1024)]
+        k_raw = []
+        for i, (u, a, b) in enumerate(pieces):
+            raw = sb.tile([P, 2, b - a], F32, name=f"k_raw{i}")
+            nc.sync.dma_start(raw[:], k_rows[:, u, :, a:b])
+            k_raw.append(raw)
+            if i == 0:
+                nc.sync.dma_start(vs_pool[0:1, :], vs[0:1, :])
+        v_pool = [sb.tile([P, T], F32, name=f"v_pool{u}") for u in range(2)]
+        nc.sync.dma_start(v_pool[0][:], vT[0:P, :])
+        nc.sync.dma_start(v_pool[1][:, 0:768], vT[P:2 * P, 0:768])
+        nc.sync.dma_start(v_pool[1][:, 768:T], vT[P:2 * P, 768:T])
+
+        q_grp = sb.tile([P, NQ, PACK], BF16, name="q_grp", align_bytes=64)
+        q_codes = sb.tile([P, NQ], U32, name="q_codes", align_bytes=64)
+        q_scales = sb.tile([P, NQ], U8, name="q_scales", align_bytes=64)
+        nc.vector.tensor_copy(q_grp[:], q_raw[:].rearrange("p j n -> p n j"))
+        nc.vector.quantize_mx(out=q_codes[:].bitcast(FP8X4), scales=q_scales[:],
+                              in_=q_grp[:].rearrange("p n j -> p (n j)"))
+
+        k_pool = [sb.tile([P, 2 * T], BF16, name=f"k_pool{u}", align_bytes=64) for u in range(2)]
+        k_grp = sb.tile([P, N * PACK], BF16, name="k_grp", align_bytes=64)
+        k_words = k_grp[:].bitcast(U32).rearrange("p (c u) -> p c u", u=2)
+        k_codes = sb.tile([P, N], U32, name="k_codes", align_bytes=64)
+        k_scales = sb.tile([P, N], U8, name="k_scales", align_bytes=64)
+
+        def cast_keys(i, scalar_share):
+            u, a, b = pieces[i]
+            pairs = k_pool[u][:].rearrange("p (n e) -> p n e", e=2)
+            src = k_raw[i][:].rearrange("p e n -> p n e")
+            if scalar_share > 0:
+                nc.scalar.activation(pairs[:, a:a + scalar_share, :], src[:, 0:scalar_share, :], ACT.Copy)
+            if scalar_share < b - a:
+                nc.vector.tensor_copy(pairs[:, a + scalar_share:b, :], src[:, scalar_share:b - a, :])
+
+        def gather_keys(u, s0, s1):
+            window = k_pool[u][:].bitcast(U32)[:, 0:T - N + s1]
+            dst = k_words[:, :, u].rearrange("p (t m) -> p m t", t=PACK)
+            nc.vector.tensor_copy(dst[:, s0 // PACK:s1 // PACK, :],
+                                  window.indirect(offsets[:, s0 // 16:s1 // 16]))
+
+        cast_keys(0, 512)
+
+        vs_g = sb.tile([P, N], F32, name="vs_g")
+        nc.vector.tensor_copy(vs_g[:], vs_pool[:].indirect(offsets[:]))
+        vs_ps = ps.tile([P, PACK, P], F32, name="vs_ps")
+        for t in range(PACK):
+            nc.tensor.transpose(vs_ps[:, t, :], vs_g[:, t:N:PACK], ident[:])
+
+        cast_keys(1, 256)
+        gather_keys(0, 0, N)
+        half_vs = sb.tile([P, PACK], F32, name="half_vs")
+        cast_keys(2, 256)
+        cast_keys(3, 128)
+        gather_keys(1, 0, HALF)
+        cast_keys(4, 128)
+        gather_keys(1, HALF, N)
+        nc.scalar.activation(half_vs[:], vs_ps[:, :, 0], ACT.Copy, scale=0.5)
+
+        score_ps = ps.tile([P, PACK, NQ], F32, name="score_ps")
+        for t2 in range(2):
+            cols = slice(t2 * 2 * P, (t2 + 1) * 2 * P)
+            nc.vector.quantize_mx(out=k_codes[:, cols].bitcast(FP8X4), scales=k_scales[:, cols],
+                                  in_=k_grp[:, t2 * 2 * P * PACK:(t2 + 1) * 2 * P * PACK])
+        for t in range(PACK):
+            cols = slice(t * P, (t + 1) * P)
+            nc.tensor.matmul_mx(out=score_ps[:, t, :], lhsT=k_codes[:, cols].bitcast(FP8X4),
+                                lhsT_scale=k_scales[:, cols], rhs=q_codes[:].bitcast(FP8X4),
+                                rhs_scale=q_scales[:], start=True, stop=True)
+
+        v_g = [sb.tile([P, N], BF16, name=f"v_g{u}", align_bytes=64) for u in range(2)]
+        v_ps = [ps.tile([P, 2, P], F32, name=f"v_ps{u}") for u in range(2)]
+        v_grp = [sb.tile([P, P * PACK], BF16, name=f"v_grp{u}", align_bytes=64) for u in range(2)]
+        v_codes = [sb.tile([P, P], U32, name=f"v_codes{u}", align_bytes=64) for u in range(2)]
+        v_scales = [sb.tile([P, P], U8, name=f"v_scales{u}", align_bytes=64) for u in range(2)]
+
+        def gather_values(u, s0, s1):
+            dst = v_g[u][:].rearrange("p (w m s) -> p m w s", w=2, s=2)
+            nc.vector.tensor_copy(dst[:, s0 // PACK:s1 // PACK],
+                                  v_pool[u][:, 0:T - N + s1].indirect(offsets[:, s0 // 16:s1 // 16]))
+
+        def turn_values(u):
+            words = v_g[u][:].bitcast(F32)
+            for w in range(2):
+                nc.tensor.transpose(v_ps[u][:, w, :], words[:, w * P:(w + 1) * P], ident[:])
+
+        gather_values(0, 0, N)
+        turn_values(0)
+        gather_values(1, 0, HALF)
+        gather_values(1, HALF, N)
+        turn_values(1)
+
+        QH = NQ // 2
+        capped = [sb.tile([P, QH, PACK], F32, name=f"capped{h}") for h in range(2)]
+        centred = [sb.tile([P, QH, PACK], F32, name=f"centred{h}") for h in range(2)]
+        w_grp = sb.tile([P, NQ, PACK], BF16, name="w_grp", align_bytes=64)
+        w_codes = sb.tile([P, NQ], U32, name="w_codes", align_bytes=64)
+        w_scales = sb.tile([P, NQ], U8, name="w_scales", align_bytes=64)
+        for h in range(2):
+            nc.scalar.activation(capped[h][:], score_ps[:, :, h * QH:(h + 1) * QH].rearrange("p t n -> p n t"),
+                                 ACT.Tanh, scale=0.5)
+        for h in range(2):
+            nc.scalar.activation(centred[h][:], capped[h][:], ACT.Tanh)
+        for u in range(2):
+            nc.scalar.copy(v_grp[u][:].bitcast(F32).rearrange("p (e w) -> p e w", w=2),
+                           v_ps[u][:].rearrange("p w e -> p e w"))
+        for h in range(2):
+            nc.vector.scalar_tensor_tensor(w_grp[:, h * QH:(h + 1) * QH, :], centred[h][:], 1.0,
+                                           half_vs[:].unsqueeze(1).to_broadcast([P, QH, PACK]),
+                                           ALU.add, ALU.mult)
+        for h in range(2):
+            cols = slice(h * QH, (h + 1) * QH)
+            nc.vector.quantize_mx(out=w_codes[:, cols].bitcast(FP8X4), scales=w_scales[:, cols],
+                                  in_=w_grp[:, cols, :].rearrange("p n t -> p (n t)"))
+
+        y_ps = [ps.tile([P, P], F32, name=f"y_ps{u}") for u in range(2)]
+        y = sb.tile([P, DV], F32, name="y")
+        for u in range(2):
+            nc.vector.quantize_mx(out=v_codes[u][:].bitcast(FP8X4), scales=v_scales[u][:],
+                                  in_=v_grp[u][:])
+        for u in range(2):
+            nc.tensor.matmul_mx(out=y_ps[u][:], lhsT=w_codes[:].bitcast(FP8X4), lhsT_scale=w_scales[:],
+                                rhs=v_codes[u][:].bitcast(FP8X4), rhs_scale=v_scales[u][:],
+                                start=True, stop=True)
+        nc.scalar.activation(y[:, 0:P], y_ps[0][:], ACT.Copy, scale=1.0 / 16.0)
+        nc.vector.tensor_scalar(y[:, P:DV], y_ps[1][:], 1.0 / 16.0, None, ALU.mult)
+        nc.sync.dma_start(out[0], y[:])

@@ -40,6 +40,7 @@ def tile_attend_x_sigmoid_cap_srt_kernel(tc, qT, kT, vT, vs, offs, out):
 
         vs_pool = sb.tile([P, T], F32, name="vs_pool")
         nc.vector.memset(vs_pool[:], 0.0)
+        nc.scalar.dma_start(vs_pool[0:1, :], vs[0:1, :])
 
         q_raw = sb.tile([P, PACK, NQ], F32, name="q_raw")
         nc.sync.dma_start(q_raw[:], qT[0].rearrange("(p j) n -> p j n", j=PACK))
@@ -50,12 +51,10 @@ def tile_attend_x_sigmoid_cap_srt_kernel(tc, qT, kT, vT, vs, offs, out):
             raw = sb.tile([P, 2, b - a], F32, name=f"k_raw{i}")
             nc.sync.dma_start(raw[:], k_rows[:, u, :, a:b])
             k_raw.append(raw)
-            if i == 0:
-                nc.sync.dma_start(vs_pool[0:1, :], vs[0:1, :])
         v_pool = [sb.tile([P, T], F32, name=f"v_pool{u}") for u in range(2)]
-        nc.sync.dma_start(v_pool[0][:], vT[0:P, :])
-        nc.sync.dma_start(v_pool[1][:, 0:768], vT[P:2 * P, 0:768])
-        nc.sync.dma_start(v_pool[1][:, 768:T], vT[P:2 * P, 768:T])
+        for u in range(2):
+            nc.sync.dma_start(v_pool[u][:, 0:768], vT[u * P:(u + 1) * P, 0:768])
+            nc.sync.dma_start(v_pool[u][:, 768:T], vT[u * P:(u + 1) * P, 768:T])
 
         q_grp = sb.tile([P, NQ, PACK], BF16, name="q_grp", align_bytes=64)
         q_codes = sb.tile([P, NQ], U32, name="q_codes", align_bytes=64)
@@ -65,8 +64,11 @@ def tile_attend_x_sigmoid_cap_srt_kernel(tc, qT, kT, vT, vs, offs, out):
                               in_=q_grp[:].rearrange("p n j -> p (n j)"))
 
         k_pool = [sb.tile([P, 2 * T], BF16, name=f"k_pool{u}", align_bytes=64) for u in range(2)]
-        k_grp = sb.tile([P, N * PACK], BF16, name="k_grp", align_bytes=64)
-        k_words = k_grp[:].bitcast(U32).rearrange("p (c u) -> p c u", u=2)
+        LEAD = 3 * N // 4
+        shared = sb.tile([P, LEAD + N * PACK], BF16, name="shared", align_bytes=64)
+        k_grp = shared[:, LEAD:]
+        v_g = [shared[:, 0:N], shared[:, N:2 * N]]
+        k_g = sb.tile([P, 2, 2 * N], BF16, name="k_g", align_bytes=64)
         k_codes = sb.tile([P, N], U32, name="k_codes", align_bytes=64)
         k_scales = sb.tile([P, N], U8, name="k_scales", align_bytes=64)
 
@@ -81,9 +83,20 @@ def tile_attend_x_sigmoid_cap_srt_kernel(tc, qT, kT, vT, vs, offs, out):
 
         def gather_keys(u, s0, s1):
             window = k_pool[u][:].bitcast(U32)[:, 0:T - N + s1]
-            dst = k_words[:, :, u].rearrange("p (t m) -> p m t", t=PACK)
+            dst = k_g[:, u, :].bitcast(U32).rearrange("p (t m) -> p m t", t=PACK)
             nc.vector.tensor_copy(dst[:, s0 // PACK:s1 // PACK, :],
                                   window.indirect(offsets[:, s0 // 16:s1 // 16]))
+
+        def join_keys(h, t0, t1):
+            src = k_g[:].bitcast(U32).rearrange("p u (t m) -> p t m u", t=PACK)
+            dst = k_grp.bitcast(U32).rearrange("p (t m u) -> p t m u", t=PACK, u=2)
+            half = slice(h * P // 2, (h + 1) * P // 2)
+            nc.scalar.copy(dst[:, t0:t1, half, :], src[:, t0:t1, half, :])
+
+        def gather_values(u, s0, s1):
+            dst = v_g[u].rearrange("p (w m s) -> p m w s", w=2, s=2)
+            nc.vector.tensor_copy(dst[:, s0 // PACK:s1 // PACK],
+                                  v_pool[u][:, 0:T - N + s1].indirect(offsets[:, s0 // 16:s1 // 16]))
 
         cast_keys(0, 512)
 
@@ -97,40 +110,38 @@ def tile_attend_x_sigmoid_cap_srt_kernel(tc, qT, kT, vT, vs, offs, out):
         gather_keys(0, 0, N)
         half_vs = sb.tile([P, PACK], F32, name="half_vs")
         cast_keys(2, 256)
-        cast_keys(3, 128)
+        cast_keys(3, 256)
         gather_keys(1, 0, HALF)
-        cast_keys(4, 128)
+        cast_keys(4, 256)
         gather_keys(1, HALF, N)
+        join_keys(0, 0, PACK)
+        join_keys(1, 2, PACK)
+        join_keys(1, 0, 2)
+        gather_values(0, 0, HALF)
         nc.scalar.activation(half_vs[:], vs_ps[:, :, 0], ACT.Copy, scale=0.5)
 
         score_ps = ps.tile([P, PACK, NQ], F32, name="score_ps")
-        for t2 in range(2):
-            cols = slice(t2 * 2 * P, (t2 + 1) * 2 * P)
+        for t in reversed(range(PACK)):
+            cols = slice(t * P, (t + 1) * P)
             nc.vector.quantize_mx(out=k_codes[:, cols].bitcast(FP8X4), scales=k_scales[:, cols],
-                                  in_=k_grp[:, t2 * 2 * P * PACK:(t2 + 1) * 2 * P * PACK])
-        for t in range(PACK):
+                                  in_=k_grp[:, t * P * PACK:(t + 1) * P * PACK])
+        for t in reversed(range(PACK)):
             cols = slice(t * P, (t + 1) * P)
             nc.tensor.matmul_mx(out=score_ps[:, t, :], lhsT=k_codes[:, cols].bitcast(FP8X4),
                                 lhsT_scale=k_scales[:, cols], rhs=q_codes[:].bitcast(FP8X4),
                                 rhs_scale=q_scales[:], start=True, stop=True)
 
-        v_g = [sb.tile([P, N], BF16, name=f"v_g{u}", align_bytes=64) for u in range(2)]
         v_ps = [ps.tile([P, 2, P], F32, name=f"v_ps{u}") for u in range(2)]
         v_grp = [sb.tile([P, P * PACK], BF16, name=f"v_grp{u}", align_bytes=64) for u in range(2)]
         v_codes = [sb.tile([P, P], U32, name=f"v_codes{u}", align_bytes=64) for u in range(2)]
         v_scales = [sb.tile([P, P], U8, name=f"v_scales{u}", align_bytes=64) for u in range(2)]
 
-        def gather_values(u, s0, s1):
-            dst = v_g[u][:].rearrange("p (w m s) -> p m w s", w=2, s=2)
-            nc.vector.tensor_copy(dst[:, s0 // PACK:s1 // PACK],
-                                  v_pool[u][:, 0:T - N + s1].indirect(offsets[:, s0 // 16:s1 // 16]))
-
         def turn_values(u):
-            words = v_g[u][:].bitcast(F32)
+            words = v_g[u].bitcast(F32)
             for w in range(2):
                 nc.tensor.transpose(v_ps[u][:, w, :], words[:, w * P:(w + 1) * P], ident[:])
 
-        gather_values(0, 0, N)
+        gather_values(0, HALF, N)
         turn_values(0)
         gather_values(1, 0, HALF)
         gather_values(1, HALF, N)
@@ -170,4 +181,5 @@ def tile_attend_x_sigmoid_cap_srt_kernel(tc, qT, kT, vT, vs, offs, out):
                                 start=True, stop=True)
         nc.scalar.activation(y[:, 0:P], y_ps[0][:], ACT.Copy, scale=1.0 / 16.0)
         nc.vector.tensor_scalar(y[:, P:DV], y_ps[1][:], 1.0 / 16.0, None, ALU.mult)
-        nc.sync.dma_start(out[0], y[:])
+        nc.scalar.dma_start(out[0, :, 0:P], y[:, 0:P])
+        nc.sync.dma_start(out[0, :, P:DV], y[:, P:DV])

@@ -28,7 +28,8 @@ def tile_attend_x_sigmoid_cap_srt_kernel(tc, qT, kT, vT, vs, offs, out):
         ps = ctx.enter_context(tc.psum_pool(name="ps", bufs=1))
 
         offsets = sb.tile([P, N // 16], U16, name="offsets")
-        nc.sync.dma_start(offsets[:], offs)
+        vs_pool = sb.tile([P, T], F32, name="vs_pool")
+        nc.gpsimd.memset(vs_pool[:], 0.0)
 
         ident = sb.tile([P, P], F32, name="ident")
         make_identity(nc, ident[:])
@@ -38,23 +39,24 @@ def tile_attend_x_sigmoid_cap_srt_kernel(tc, qT, kT, vT, vs, offs, out):
         nc.vector.memset(warm_in[:], 0.0)
         nc.scalar.activation(warm[:], warm_in[:], ACT.Tanh)
 
-        vs_pool = sb.tile([P, T], F32, name="vs_pool")
-        nc.vector.memset(vs_pool[:], 0.0)
-        nc.scalar.dma_start(vs_pool[0:1, :], vs[0:1, :])
 
         q_raw = sb.tile([P, PACK, NQ], F32, name="q_raw")
         nc.sync.dma_start(q_raw[:], qT[0].rearrange("(p j) n -> p j n", j=PACK))
+        nc.sync.dma_start(offsets[:], offs)
         k_rows = kT.rearrange("(p u e) n -> p u e n", u=2, e=2)
-        pieces = [(0, 0, 512), (0, 512, 1024), (1, 0, 512), (1, 512, 768), (1, 768, 1024)]
+        pieces = [(0, 0, 384), (0, 384, T), (1, 0, 768), (1, 768, T)]
         k_raw = []
         for i, (u, a, b) in enumerate(pieces):
-            raw = sb.tile([P, 2, b - a], F32, name=f"k_raw{i}")
+            raw = sb.tile([P, 2, b - a], F32, name=f"k_raw{i}", tag=f"k_raw{i}", align_bytes=64)
             nc.sync.dma_start(raw[:], k_rows[:, u, :, a:b])
             k_raw.append(raw)
-        v_pool = [sb.tile([P, T], F32, name=f"v_pool{u}") for u in range(2)]
+            if i == 0:
+                nc.sync.dma_start(vs_pool[0:1, :], vs[0:1, :])
+        v_pool = sb.tile([P, 2, T], F32, name="v_pool")
+        v_rows = vT.rearrange("(u p) n -> p u n", u=2)
         for u in range(2):
-            nc.sync.dma_start(v_pool[u][:, 0:768], vT[u * P:(u + 1) * P, 0:768])
-            nc.sync.dma_start(v_pool[u][:, 768:T], vT[u * P:(u + 1) * P, 768:T])
+            nc.sync.dma_start(v_pool[:, u, 0:768], v_rows[:, u, 0:768])
+        nc.sync.dma_start(v_pool[:, :, 768:T], v_rows[:, :, 768:T])
 
         q_grp = sb.tile([P, NQ, PACK], BF16, name="q_grp", align_bytes=64)
         q_codes = sb.tile([P, NQ], U32, name="q_codes", align_bytes=64)
@@ -63,9 +65,10 @@ def tile_attend_x_sigmoid_cap_srt_kernel(tc, qT, kT, vT, vs, offs, out):
         nc.vector.quantize_mx(out=q_codes[:].bitcast(FP8X4), scales=q_scales[:],
                               in_=q_grp[:].rearrange("p n j -> p (n j)"))
 
-        k_pool = [sb.tile([P, 2 * T], BF16, name=f"k_pool{u}", align_bytes=64) for u in range(2)]
+        k_pool = [sb.tile([P, 2 * T], BF16, name="k_pool0", align_bytes=64),
+                  sb.tile([P, 2 * T], BF16, name="k_pool1", tag="k_raw1", align_bytes=64)]
         LEAD = 3 * N // 4
-        shared = sb.tile([P, LEAD + N * PACK], BF16, name="shared", align_bytes=64)
+        shared = sb.tile([P, LEAD + N * PACK], BF16, name="shared", tag="k_raw3", align_bytes=64)
         k_grp = shared[:, LEAD:]
         v_g = [shared[:, 0:N], shared[:, N:2 * N]]
         k_g = sb.tile([P, 2, 2 * N], BF16, name="k_g", align_bytes=64)
@@ -96,9 +99,10 @@ def tile_attend_x_sigmoid_cap_srt_kernel(tc, qT, kT, vT, vs, offs, out):
         def gather_values(u, s0, s1):
             dst = v_g[u].rearrange("p (w m s) -> p m w s", w=2, s=2)
             nc.vector.tensor_copy(dst[:, s0 // PACK:s1 // PACK],
-                                  v_pool[u][:, 0:T - N + s1].indirect(offsets[:, s0 // 16:s1 // 16]))
+                                  v_pool[:, u, 0:T - N + s1].indirect(offsets[:, s0 // 16:s1 // 16]))
 
-        cast_keys(0, 512)
+
+        cast_keys(0, 384)
 
         vs_g = sb.tile([P, N], F32, name="vs_g")
         nc.vector.tensor_copy(vs_g[:], vs_pool[:].indirect(offsets[:]))
@@ -106,13 +110,12 @@ def tile_attend_x_sigmoid_cap_srt_kernel(tc, qT, kT, vT, vs, offs, out):
         for t in range(PACK):
             nc.tensor.transpose(vs_ps[:, t, :], vs_g[:, t:N:PACK], ident[:])
 
-        cast_keys(1, 256)
+        cast_keys(1, 224)
         gather_keys(0, 0, N)
         half_vs = sb.tile([P, PACK], F32, name="half_vs")
-        cast_keys(2, 256)
-        cast_keys(3, 256)
+        cast_keys(2, 320)
         gather_keys(1, 0, HALF)
-        cast_keys(4, 256)
+        cast_keys(3, 256)
         gather_keys(1, HALF, N)
         join_keys(0, 0, PACK)
         join_keys(1, 2, PACK)
@@ -141,9 +144,9 @@ def tile_attend_x_sigmoid_cap_srt_kernel(tc, qT, kT, vT, vs, offs, out):
             for w in range(2):
                 nc.tensor.transpose(v_ps[u][:, w, :], words[:, w * P:(w + 1) * P], ident[:])
 
+        gather_values(1, 0, HALF)
         gather_values(0, HALF, N)
         turn_values(0)
-        gather_values(1, 0, HALF)
         gather_values(1, HALF, N)
         turn_values(1)
 

@@ -29,7 +29,8 @@ def tile_attend_x_sigmoid_cap_srt_kernel(tc, qT, kT, vT, vs, offs, out):
 
         offsets = sb.tile([P, N // 16], U16, name="offsets")
         vs_pool = sb.tile([P, T], F32, name="vs_pool")
-        nc.gpsimd.memset(vs_pool[:], 0.0)
+        nc.gpsimd.memset(vs_pool[:, 0:T // 2], 0.0)
+        nc.vector.memset(vs_pool[:, T // 2:T], 0.0)
 
         ident = sb.tile([P, P], F32, name="ident")
         make_identity(nc, ident[:])
@@ -41,36 +42,31 @@ def tile_attend_x_sigmoid_cap_srt_kernel(tc, qT, kT, vT, vs, offs, out):
 
 
         q_raw = sb.tile([P, PACK, NQ], F32, name="q_raw")
-        nc.sync.dma_start(q_raw[:], qT[0].rearrange("(p j) n -> p j n", j=PACK))
-        nc.sync.dma_start(offsets[:], offs)
         k_rows = kT.rearrange("(p u e) n -> p u e n", u=2, e=2)
-        pieces = [(0, 0, 384), (0, 384, T), (1, 0, 768), (1, 768, T)]
+        pieces = [(0, 0, 512), (0, 512, T), (1, 0, 768), (1, 768, T)]
         k_raw = []
         for i, (u, a, b) in enumerate(pieces):
             raw = sb.tile([P, 2, b - a], F32, name=f"k_raw{i}", tag=f"k_raw{i}", align_bytes=64)
             nc.sync.dma_start(raw[:], k_rows[:, u, :, a:b])
             k_raw.append(raw)
             if i == 0:
+                nc.sync.dma_start(offsets[:], offs)
                 nc.sync.dma_start(vs_pool[0:1, :], vs[0:1, :])
-        v_pool = sb.tile([P, 2, T], F32, name="v_pool")
-        v_rows = vT.rearrange("(u p) n -> p u n", u=2)
+            if i == 1:
+                nc.sync.dma_start(q_raw[:], qT[0].rearrange("(p j) n -> p j n", j=PACK))
+        v_pool = [sb.tile([P, T], F32, name=f"v_pool{u}") for u in range(2)]
         for u in range(2):
-            nc.sync.dma_start(v_pool[:, u, 0:768], v_rows[:, u, 0:768])
-        nc.sync.dma_start(v_pool[:, :, 768:T], v_rows[:, :, 768:T])
+            nc.sync.dma_start(v_pool[u][:], vT[u * P:(u + 1) * P, :])
 
         q_grp = sb.tile([P, NQ, PACK], BF16, name="q_grp", align_bytes=64)
         q_codes = sb.tile([P, NQ], U32, name="q_codes", align_bytes=64)
         q_scales = sb.tile([P, NQ], U8, name="q_scales", align_bytes=64)
-        nc.vector.tensor_copy(q_grp[:], q_raw[:].rearrange("p j n -> p n j"))
-        nc.vector.quantize_mx(out=q_codes[:].bitcast(FP8X4), scales=q_scales[:],
-                              in_=q_grp[:].rearrange("p n j -> p (n j)"))
 
         k_pool = [sb.tile([P, 2 * T], BF16, name="k_pool0", align_bytes=64),
                   sb.tile([P, 2 * T], BF16, name="k_pool1", tag="k_raw1", align_bytes=64)]
-        LEAD = 3 * N // 4
-        shared = sb.tile([P, LEAD + N * PACK], BF16, name="shared", tag="k_raw3", align_bytes=64)
-        k_grp = shared[:, LEAD:]
-        v_g = [shared[:, 0:N], shared[:, N:2 * N]]
+        k_grp = sb.tile([P, N * PACK], BF16, name="k_grp", align_bytes=64)
+        v_g0 = sb.tile([P, N], BF16, name="v_g0", align_bytes=64)
+        v_g = [v_g0[:], k_grp[:, 0:N]]
         k_g = sb.tile([P, 2, 2 * N], BF16, name="k_g", align_bytes=64)
         k_codes = sb.tile([P, N], U32, name="k_codes", align_bytes=64)
         k_scales = sb.tile([P, N], U8, name="k_scales", align_bytes=64)
@@ -92,17 +88,15 @@ def tile_attend_x_sigmoid_cap_srt_kernel(tc, qT, kT, vT, vs, offs, out):
 
         def join_keys(h, t0, t1):
             src = k_g[:].bitcast(U32).rearrange("p u (t m) -> p t m u", t=PACK)
-            dst = k_grp.bitcast(U32).rearrange("p (t m u) -> p t m u", t=PACK, u=2)
+            dst = k_grp[:].bitcast(U32).rearrange("p (t m u) -> p t m u", t=PACK, u=2)
             half = slice(h * P // 2, (h + 1) * P // 2)
             nc.scalar.copy(dst[:, t0:t1, half, :], src[:, t0:t1, half, :])
 
-        def gather_values(u, s0, s1):
-            dst = v_g[u].rearrange("p (w m s) -> p m w s", w=2, s=2)
-            nc.vector.tensor_copy(dst[:, s0 // PACK:s1 // PACK],
-                                  v_pool[:, u, 0:T - N + s1].indirect(offsets[:, s0 // 16:s1 // 16]))
+        def slot_pairs(u):
+            return v_g[u].rearrange("p (w m s) -> p m w s", w=2, s=2)
 
 
-        cast_keys(0, 384)
+        cast_keys(0, 512)
 
         vs_g = sb.tile([P, N], F32, name="vs_g")
         nc.vector.tensor_copy(vs_g[:], vs_pool[:].indirect(offsets[:]))
@@ -110,17 +104,21 @@ def tile_attend_x_sigmoid_cap_srt_kernel(tc, qT, kT, vT, vs, offs, out):
         for t in range(PACK):
             nc.tensor.transpose(vs_ps[:, t, :], vs_g[:, t:N:PACK], ident[:])
 
-        cast_keys(1, 224)
+        cast_keys(1, 192)
         gather_keys(0, 0, N)
+        nc.scalar.activation(q_grp[:], q_raw[:].rearrange("p j n -> p n j"), ACT.Copy)
+        nc.vector.quantize_mx(out=q_codes[:].bitcast(FP8X4), scales=q_scales[:],
+                              in_=q_grp[:].rearrange("p n j -> p (n j)"))
         half_vs = sb.tile([P, PACK], F32, name="half_vs")
-        cast_keys(2, 320)
+        cast_keys(2, 256)
         gather_keys(1, 0, HALF)
         cast_keys(3, 256)
         gather_keys(1, HALF, N)
         join_keys(0, 0, PACK)
         join_keys(1, 2, PACK)
         join_keys(1, 0, 2)
-        gather_values(0, 0, HALF)
+        v_bf = sb.tile([P, T], BF16, name="v_bf", tag="k_raw3", align_bytes=64)
+        nc.vector.tensor_copy(v_bf[:], v_pool[0][:])
         nc.scalar.activation(half_vs[:], vs_ps[:, :, 0], ACT.Copy, scale=0.5)
 
         score_ps = ps.tile([P, PACK, NQ], F32, name="score_ps")
@@ -144,11 +142,19 @@ def tile_attend_x_sigmoid_cap_srt_kernel(tc, qT, kT, vT, vs, offs, out):
             for w in range(2):
                 nc.tensor.transpose(v_ps[u][:, w, :], words[:, w * P:(w + 1) * P], ident[:])
 
-        gather_values(1, 0, HALF)
-        gather_values(0, HALF, N)
+        nc.scalar.activation(slot_pairs(0), v_bf[:].indirect(offsets[:]), ACT.Copy)
         turn_values(0)
-        gather_values(1, HALF, N)
+        nc.vector.tensor_copy(slot_pairs(1), v_pool[1][:].indirect(offsets[:]))
         turn_values(1)
+
+        def pack_values(copy, u):
+            copy(v_grp[u][:].bitcast(F32).rearrange("p (e w) -> p e w", w=2),
+                 v_ps[u][:].rearrange("p w e -> p e w"))
+
+        def quantize_values(u):
+            nc.vector.quantize_mx(out=v_codes[u][:].bitcast(FP8X4), scales=v_scales[u][:], in_=v_grp[u][:])
+
+        pack_values(nc.vector.tensor_copy, 0)
 
         QH = NQ // 2
         capped = [sb.tile([P, QH, PACK], F32, name=f"capped{h}") for h in range(2)]
@@ -161,28 +167,32 @@ def tile_attend_x_sigmoid_cap_srt_kernel(tc, qT, kT, vT, vs, offs, out):
                                  ACT.Tanh, scale=0.5)
         for h in range(2):
             nc.scalar.activation(centred[h][:], capped[h][:], ACT.Tanh)
-        for u in range(2):
-            nc.scalar.copy(v_grp[u][:].bitcast(F32).rearrange("p (e w) -> p e w", w=2),
-                           v_ps[u][:].rearrange("p w e -> p e w"))
-        for h in range(2):
+        pack_values(nc.scalar.copy, 1)
+
+        def weigh(h):
             nc.vector.scalar_tensor_tensor(w_grp[:, h * QH:(h + 1) * QH, :], centred[h][:], 1.0,
                                            half_vs[:].unsqueeze(1).to_broadcast([P, QH, PACK]),
                                            ALU.add, ALU.mult)
-        for h in range(2):
+
+        def quantize_weights(h):
             cols = slice(h * QH, (h + 1) * QH)
             nc.vector.quantize_mx(out=w_codes[:, cols].bitcast(FP8X4), scales=w_scales[:, cols],
                                   in_=w_grp[:, cols, :].rearrange("p n t -> p (n t)"))
 
+        weigh(0)
+        quantize_values(0)
+        weigh(1)
+        quantize_weights(0)
+        quantize_weights(1)
+        quantize_values(1)
+
         y_ps = [ps.tile([P, P], F32, name=f"y_ps{u}") for u in range(2)]
         y = sb.tile([P, DV], F32, name="y")
-        for u in range(2):
-            nc.vector.quantize_mx(out=v_codes[u][:].bitcast(FP8X4), scales=v_scales[u][:],
-                                  in_=v_grp[u][:])
         for u in range(2):
             nc.tensor.matmul_mx(out=y_ps[u][:], lhsT=w_codes[:].bitcast(FP8X4), lhsT_scale=w_scales[:],
                                 rhs=v_codes[u][:].bitcast(FP8X4), rhs_scale=v_scales[u][:],
                                 start=True, stop=True)
-        nc.scalar.activation(y[:, 0:P], y_ps[0][:], ACT.Copy, scale=1.0 / 16.0)
-        nc.vector.tensor_scalar(y[:, P:DV], y_ps[1][:], 1.0 / 16.0, None, ALU.mult)
-        nc.scalar.dma_start(out[0, :, 0:P], y[:, 0:P])
-        nc.sync.dma_start(out[0, :, P:DV], y[:, P:DV])
+        nc.vector.tensor_scalar(y[:, 0:P], y_ps[0][:], 1.0 / 16.0, None, ALU.mult)
+        nc.scalar.activation(y[:, P:DV], y_ps[1][:], ACT.Copy, scale=1.0 / 16.0)
+        nc.sync.dma_start(out[0, :, 0:P], y[:, 0:P])
+        nc.scalar.dma_start(out[0, :, P:DV], y[:, P:DV])

@@ -115,8 +115,8 @@ def tile_attend_x_sigmoid_cap_srt_kernel(tc, qT, kT, vT, vs, offs, out):
         cast_keys(3, 256)
         gather_keys(1, HALF, N)
         join_keys(0, 0, PACK)
-        join_keys(1, 2, PACK)
-        join_keys(1, 0, 2)
+        for t in reversed(range(PACK)):
+            join_keys(1, t, t + 1)
         v_bf = sb.tile([P, T], BF16, name="v_bf", tag="k_raw3", align_bytes=64)
         nc.vector.tensor_copy(v_bf[:], v_pool[0][:])
         nc.scalar.activation(half_vs[:], vs_ps[:, :, 0], ACT.Copy, scale=0.5)
@@ -155,6 +155,7 @@ def tile_attend_x_sigmoid_cap_srt_kernel(tc, qT, kT, vT, vs, offs, out):
             nc.vector.quantize_mx(out=v_codes[u][:].bitcast(FP8X4), scales=v_scales[u][:], in_=v_grp[u][:])
 
         pack_values(nc.vector.tensor_copy, 0)
+        quantize_values(0)
 
         QH = NQ // 2
         capped = [sb.tile([P, QH, PACK], F32, name=f"capped{h}") for h in range(2)]
@@ -180,11 +181,10 @@ def tile_attend_x_sigmoid_cap_srt_kernel(tc, qT, kT, vT, vs, offs, out):
                                   in_=w_grp[:, cols, :].rearrange("p n t -> p (n t)"))
 
         weigh(0)
-        quantize_values(0)
         weigh(1)
         quantize_weights(0)
-        quantize_weights(1)
         quantize_values(1)
+        quantize_weights(1)
 
         y_ps = [ps.tile([P, P], F32, name=f"y_ps{u}") for u in range(2)]
         y = sb.tile([P, DV], F32, name="y")

@@ -10,6 +10,7 @@ BYTES = 4 * (D * NQ + D * T + DV * T + T + NQ * DV) + 2 * 128 * (N // 16)
 F32 = mybir.dt.float32
 BF16 = mybir.dt.bfloat16
 U32 = mybir.dt.uint32
+I32 = mybir.dt.int32
 U16 = mybir.dt.uint16
 U8 = mybir.dt.uint8
 FP8X4 = mybir.dt.float8_e4m3fn_x4
@@ -29,41 +30,38 @@ def tile_attend_x_sigmoid_cap_srt_kernel(tc, qT, kT, vT, vs, offs, out):
 
         offsets = sb.tile([P, N // 16], U16, name="offsets")
         vs_pool = sb.tile([P, T], F32, name="vs_pool")
-        nc.gpsimd.memset(vs_pool[:, 0:T // 2], 0.0)
-        nc.vector.memset(vs_pool[:, T // 2:T], 0.0)
+        nc.gpsimd.memset(vs_pool[0:P - 1, 0:T // 2], 0.0)
+        nc.vector.memset(vs_pool[0:P - 1, T // 2:T], 0.0)
 
         ident = sb.tile([P, P], F32, name="ident")
         make_identity(nc, ident[:])
+
+        q_raw = sb.tile([P, PACK, NQ], F32, name="q_raw")
+        k_rows = kT.rearrange("(p u e) n -> p u e n", u=2, e=2)
+        pieces = [(0, 0, T), (1, 0, 768), (1, 768, T)]
+        k_raw = []
+        nc.scalar.dma_start(vs_pool[P - 1:P, :], vs[0:1, :])
+        nc.sync.dma_start(q_raw[:], qT[0].rearrange("(p j) n -> p j n", j=PACK))
+        nc.sync.dma_start(offsets[:], offs)
+        for i, (u, a, b) in enumerate(pieces):
+            raw = sb.tile([P, 2, b - a], F32, name=f"k_raw{i}", tag=f"k_raw{i}", align_bytes=64)
+            nc.sync.dma_start(raw[:], k_rows[:, u, :, a:b])
+            k_raw.append(raw)
+        v_pool = [sb.tile([P, T], F32, name=f"v_pool{u}") for u in range(2)]
+        for u in range(2):
+            nc.sync.dma_start(v_pool[u][:], vT[u * P:(u + 1) * P, :])
 
         warm_in = sb.tile([P, 8], F32, name="warm_in")
         warm = sb.tile([P, 8], F32, name="warm")
         nc.vector.memset(warm_in[:], 0.0)
         nc.scalar.activation(warm[:], warm_in[:], ACT.Tanh)
 
-
-        q_raw = sb.tile([P, PACK, NQ], F32, name="q_raw")
-        k_rows = kT.rearrange("(p u e) n -> p u e n", u=2, e=2)
-        pieces = [(0, 0, 512), (0, 512, T), (1, 0, 768), (1, 768, T)]
-        k_raw = []
-        for i, (u, a, b) in enumerate(pieces):
-            raw = sb.tile([P, 2, b - a], F32, name=f"k_raw{i}", tag=f"k_raw{i}", align_bytes=64)
-            nc.sync.dma_start(raw[:], k_rows[:, u, :, a:b])
-            k_raw.append(raw)
-            if i == 0:
-                nc.sync.dma_start(offsets[:], offs)
-                nc.sync.dma_start(vs_pool[0:1, :], vs[0:1, :])
-            if i == 1:
-                nc.sync.dma_start(q_raw[:], qT[0].rearrange("(p j) n -> p j n", j=PACK))
-        v_pool = [sb.tile([P, T], F32, name=f"v_pool{u}") for u in range(2)]
-        for u in range(2):
-            nc.sync.dma_start(v_pool[u][:], vT[u * P:(u + 1) * P, :])
-
         q_grp = sb.tile([P, NQ, PACK], BF16, name="q_grp", align_bytes=64)
         q_codes = sb.tile([P, NQ], U32, name="q_codes", align_bytes=64)
         q_scales = sb.tile([P, NQ], U8, name="q_scales", align_bytes=64)
 
         k_pool = [sb.tile([P, 2 * T], BF16, name="k_pool0", align_bytes=64),
-                  sb.tile([P, 2 * T], BF16, name="k_pool1", tag="k_raw1", align_bytes=64)]
+                  sb.tile([P, 2 * T], BF16, name="k_pool1", tag="k_raw0", align_bytes=64)]
         k_grp = sb.tile([P, N * PACK], BF16, name="k_grp", align_bytes=64)
         v_g0 = sb.tile([P, N], BF16, name="v_g0", align_bytes=64)
         v_g = [v_g0[:], k_grp[:, 0:N]]
@@ -71,14 +69,14 @@ def tile_attend_x_sigmoid_cap_srt_kernel(tc, qT, kT, vT, vs, offs, out):
         k_codes = sb.tile([P, N], U32, name="k_codes", align_bytes=64)
         k_scales = sb.tile([P, N], U8, name="k_scales", align_bytes=64)
 
-        def cast_keys(i, scalar_share):
+        def cast_keys(on_scalar, i, n0, n1):
             u, a, b = pieces[i]
-            pairs = k_pool[u][:].rearrange("p (n e) -> p n e", e=2)
-            src = k_raw[i][:].rearrange("p e n -> p n e")
-            if scalar_share > 0:
-                nc.scalar.activation(pairs[:, a:a + scalar_share, :], src[:, 0:scalar_share, :], ACT.Copy)
-            if scalar_share < b - a:
-                nc.vector.tensor_copy(pairs[:, a + scalar_share:b, :], src[:, scalar_share:b - a, :])
+            pairs = k_pool[u][:].rearrange("p (n e) -> p n e", e=2)[:, n0:n1, :]
+            src = k_raw[i][:].rearrange("p e n -> p n e")[:, n0 - a:n1 - a, :]
+            if on_scalar:
+                nc.scalar.activation(pairs, src, ACT.Copy)
+            else:
+                nc.vector.tensor_copy(pairs, src)
 
         def gather_keys(u, s0, s1):
             window = k_pool[u][:].bitcast(U32)[:, 0:T - N + s1]
@@ -96,30 +94,32 @@ def tile_attend_x_sigmoid_cap_srt_kernel(tc, qT, kT, vT, vs, offs, out):
             return v_g[u].rearrange("p (w m s) -> p m w s", w=2, s=2)
 
 
-        cast_keys(0, 512)
-
         vs_g = sb.tile([P, N], F32, name="vs_g")
         nc.vector.tensor_copy(vs_g[:], vs_pool[:].indirect(offsets[:]))
         vs_ps = ps.tile([P, PACK, P], F32, name="vs_ps")
         for t in range(PACK):
             nc.tensor.transpose(vs_ps[:, t, :], vs_g[:, t:N:PACK], ident[:])
 
-        cast_keys(1, 192)
-        gather_keys(0, 0, N)
         nc.scalar.activation(q_grp[:], q_raw[:].rearrange("p j n -> p n j"), ACT.Copy)
         nc.vector.quantize_mx(out=q_codes[:].bitcast(FP8X4), scales=q_scales[:],
                               in_=q_grp[:].rearrange("p n j -> p (n j)"))
+        cast_keys(False, 0, 0, 576)
+        cast_keys(True, 0, 576, 768)
+        cast_keys(True, 0, 768, T)
+        gather_keys(0, 0, HALF)
+        gather_keys(0, HALF, N)
         half_vs = sb.tile([P, PACK], F32, name="half_vs")
-        cast_keys(2, 256)
+        cast_keys(True, 1, 0, 320)
+        cast_keys(False, 1, 320, 768)
         gather_keys(1, 0, HALF)
-        cast_keys(3, 256)
+        cast_keys(True, 2, 768, T)
         gather_keys(1, HALF, N)
         join_keys(0, 0, PACK)
         for t in reversed(range(PACK)):
             join_keys(1, t, t + 1)
-        v_bf = sb.tile([P, T], BF16, name="v_bf", tag="k_raw3", align_bytes=64)
+        v_bf = sb.tile([P, T], BF16, name="v_bf", tag="k_raw2", align_bytes=64)
         nc.vector.tensor_copy(v_bf[:], v_pool[0][:])
-        nc.scalar.activation(half_vs[:], vs_ps[:, :, 0], ACT.Copy, scale=0.5)
+        nc.scalar.activation(half_vs[:], vs_ps[:, :, P - 1], ACT.Copy, scale=0.5)
 
         score_ps = ps.tile([P, PACK, NQ], F32, name="score_ps")
         for t in reversed(range(PACK)):

@@ -62,9 +62,11 @@ def tile_attend_x_sigmoid_cap_srt_kernel(tc, qT, kT, vT, vs, offs, out):
 
         k_pool = [sb.tile([P, 2 * T], BF16, name="k_pool0", align_bytes=64),
                   sb.tile([P, 2 * T], BF16, name="k_pool1", tag="k_raw0", align_bytes=64)]
-        k_grp = sb.tile([P, N * PACK], BF16, name="k_grp", align_bytes=64)
-        v_g0 = sb.tile([P, N], BF16, name="v_g0", align_bytes=64)
-        v_g = [v_g0[:], k_grp[:, 0:N]]
+        SHARE = 320
+        lead = HALF + SHARE // 2
+        late = sb.tile([P, lead + N * PACK], BF16, name="late", align_bytes=64)
+        k_grp = late[:, lead:lead + N * PACK]
+        v_g = [late[:, 0:N], late[:, N:2 * N]]
         k_g = sb.tile([P, 2, 2 * N], BF16, name="k_g", align_bytes=64)
         k_codes = sb.tile([P, N], U32, name="k_codes", align_bytes=64)
         k_scales = sb.tile([P, N], U8, name="k_scales", align_bytes=64)
@@ -86,12 +88,12 @@ def tile_attend_x_sigmoid_cap_srt_kernel(tc, qT, kT, vT, vs, offs, out):
 
         def join_keys(h, t0, t1):
             src = k_g[:].bitcast(U32).rearrange("p u (t m) -> p t m u", t=PACK)
-            dst = k_grp[:].bitcast(U32).rearrange("p (t m u) -> p t m u", t=PACK, u=2)
+            dst = k_grp.bitcast(U32).rearrange("p (t m u) -> p t m u", t=PACK, u=2)
             half = slice(h * P // 2, (h + 1) * P // 2)
             nc.scalar.copy(dst[:, t0:t1, half, :], src[:, t0:t1, half, :])
 
-        def slot_pairs(u):
-            return v_g[u].rearrange("p (w m s) -> p m w s", w=2, s=2)
+        def slot_pairs(u, s0, s1):
+            return v_g[u].rearrange("p (w m s) -> p m w s", w=2, s=2)[:, s0 // PACK:s1 // PACK, :, :]
 
 
         vs_g = sb.tile([P, N], F32, name="vs_g")
@@ -109,32 +111,31 @@ def tile_attend_x_sigmoid_cap_srt_kernel(tc, qT, kT, vT, vs, offs, out):
         gather_keys(0, 0, HALF)
         gather_keys(0, HALF, N)
         half_vs = sb.tile([P, PACK], F32, name="half_vs")
-        cast_keys(True, 1, 0, 320)
-        cast_keys(False, 1, 320, 768)
+        cast_keys(True, 1, 0, 288)
+        cast_keys(False, 1, 288, 768)
         gather_keys(1, 0, HALF)
         cast_keys(True, 2, 768, T)
         gather_keys(1, HALF, N)
         join_keys(0, 0, PACK)
         for t in reversed(range(PACK)):
             join_keys(1, t, t + 1)
-        v_bf = sb.tile([P, T], BF16, name="v_bf", tag="k_raw2", align_bytes=64)
-        nc.vector.tensor_copy(v_bf[:], v_pool[0][:])
+        v_bf = sb.tile([P, T - N + SHARE], BF16, name="v_bf", tag="k_raw2", align_bytes=64)
+        nc.vector.tensor_copy(v_bf[:], v_pool[0][:, 0:T - N + SHARE])
         nc.scalar.activation(half_vs[:], vs_ps[:, :, P - 1], ACT.Copy, scale=0.5)
 
-        score_ps = ps.tile([P, PACK, NQ], F32, name="score_ps")
+        score_ps = [ps.tile([P, 2, NQ], F32, name=f"score_ps{i}") for i in range(2)]
         for t in reversed(range(PACK)):
             cols = slice(t * P, (t + 1) * P)
             nc.vector.quantize_mx(out=k_codes[:, cols].bitcast(FP8X4), scales=k_scales[:, cols],
                                   in_=k_grp[:, t * P * PACK:(t + 1) * P * PACK])
         for t in reversed(range(PACK)):
             cols = slice(t * P, (t + 1) * P)
-            nc.tensor.matmul_mx(out=score_ps[:, t, :], lhsT=k_codes[:, cols].bitcast(FP8X4),
+            nc.tensor.matmul_mx(out=score_ps[t // 2][:, t % 2, :], lhsT=k_codes[:, cols].bitcast(FP8X4),
                                 lhsT_scale=k_scales[:, cols], rhs=q_codes[:].bitcast(FP8X4),
                                 rhs_scale=q_scales[:], start=True, stop=True)
 
         v_ps = [ps.tile([P, 2, P], F32, name=f"v_ps{u}") for u in range(2)]
         v_grp = [sb.tile([P, P * PACK], BF16, name=f"v_grp{u}", align_bytes=64) for u in range(2)]
-        v_codes = [sb.tile([P, P], U32, name=f"v_codes{u}", align_bytes=64) for u in range(2)]
         v_scales = [sb.tile([P, P], U8, name=f"v_scales{u}", align_bytes=64) for u in range(2)]
 
         def turn_values(u):
@@ -142,9 +143,10 @@ def tile_attend_x_sigmoid_cap_srt_kernel(tc, qT, kT, vT, vs, offs, out):
             for w in range(2):
                 nc.tensor.transpose(v_ps[u][:, w, :], words[:, w * P:(w + 1) * P], ident[:])
 
-        nc.scalar.activation(slot_pairs(0), v_bf[:].indirect(offsets[:]), ACT.Copy)
+        nc.scalar.activation(slot_pairs(0, 0, SHARE), v_bf[:].indirect(offsets[:, 0:SHARE // 16]), ACT.Copy)
+        nc.vector.tensor_copy(slot_pairs(0, SHARE, N), v_pool[0][:].indirect(offsets[:, SHARE // 16:N // 16]))
         turn_values(0)
-        nc.vector.tensor_copy(slot_pairs(1), v_pool[1][:].indirect(offsets[:]))
+        nc.vector.tensor_copy(slot_pairs(1, 0, N), v_pool[1][:].indirect(offsets[:]))
         turn_values(1)
 
         def pack_values(copy, u):
@@ -155,24 +157,32 @@ def tile_attend_x_sigmoid_cap_srt_kernel(tc, qT, kT, vT, vs, offs, out):
             nc.vector.quantize_mx(out=v_codes[u][:].bitcast(FP8X4), scales=v_scales[u][:], in_=v_grp[u][:])
 
         pack_values(nc.vector.tensor_copy, 0)
-        quantize_values(0)
 
         QH = NQ // 2
-        capped = [sb.tile([P, QH, PACK], F32, name=f"capped{h}") for h in range(2)]
-        centred = [sb.tile([P, QH, PACK], F32, name=f"centred{h}") for h in range(2)]
+        capped = sb.tile([P, 2, NQ, 2], F32, name="capped", tag="capped", align_bytes=64)
+        QQ = NQ // 4
+        centred = [sb.tile([P, QQ, PACK], F32, name=f"centred{c}") for c in range(4)]
+        v_codes = [sb.tile([P, P], U32, name="v_codes0", tag="capped", align_bytes=64),
+                   sb.tile([P, P], U32, name="v_codes1", align_bytes=64)]
         w_grp = sb.tile([P, NQ, PACK], BF16, name="w_grp", align_bytes=64)
         w_codes = sb.tile([P, NQ], U32, name="w_codes", align_bytes=64)
         w_scales = sb.tile([P, NQ], U8, name="w_scales", align_bytes=64)
-        for h in range(2):
-            nc.scalar.activation(capped[h][:], score_ps[:, :, h * QH:(h + 1) * QH].rearrange("p t n -> p n t"),
+
+        def cap(i, q0, q1):
+            nc.scalar.activation(capped[:, i, q0:q1, :], score_ps[i][:, :, q0:q1].rearrange("p s n -> p n s"),
                                  ACT.Tanh, scale=0.5)
-        for h in range(2):
-            nc.scalar.activation(centred[h][:], capped[h][:], ACT.Tanh)
+
+        cap(1, 0, NQ)
+        cap(0, 0, QH)
+        cap(0, QH, NQ)
+        for c in range(4):
+            nc.scalar.activation(centred[c][:].rearrange("p n (i s) -> p n i s", i=2),
+                                 capped[:, :, c * QQ:(c + 1) * QQ, :].rearrange("p i n s -> p n i s"), ACT.Tanh)
         pack_values(nc.scalar.copy, 1)
 
-        def weigh(h):
-            nc.vector.scalar_tensor_tensor(w_grp[:, h * QH:(h + 1) * QH, :], centred[h][:], 1.0,
-                                           half_vs[:].unsqueeze(1).to_broadcast([P, QH, PACK]),
+        def weigh(c):
+            nc.vector.scalar_tensor_tensor(w_grp[:, c * QQ:(c + 1) * QQ, :], centred[c][:], 1.0,
+                                           half_vs[:].unsqueeze(1).to_broadcast([P, QQ, PACK]),
                                            ALU.add, ALU.mult)
 
         def quantize_weights(h):
@@ -180,11 +190,12 @@ def tile_attend_x_sigmoid_cap_srt_kernel(tc, qT, kT, vT, vs, offs, out):
             nc.vector.quantize_mx(out=w_codes[:, cols].bitcast(FP8X4), scales=w_scales[:, cols],
                                   in_=w_grp[:, cols, :].rearrange("p n t -> p (n t)"))
 
-        weigh(0)
-        weigh(1)
+        for c in range(4):
+            weigh(c)
         quantize_weights(0)
-        quantize_values(1)
+        quantize_values(0)
         quantize_weights(1)
+        quantize_values(1)
 
         y_ps = [ps.tile([P, P], F32, name=f"y_ps{u}") for u in range(2)]
         y = sb.tile([P, DV], F32, name="y")

@@ -62,7 +62,7 @@ def tile_attend_x_sigmoid_cap_srt_kernel(tc, qT, kT, vT, vs, offs, out):
 
         k_pool = [sb.tile([P, 2 * T], BF16, name="k_pool0", align_bytes=64),
                   sb.tile([P, 2 * T], BF16, name="k_pool1", tag="k_raw0", align_bytes=64)]
-        SHARE = 320
+        SHARE = 384
         lead = HALF + SHARE // 2
         late = sb.tile([P, lead + N * PACK], BF16, name="late", align_bytes=64)
         k_grp = late[:, lead:lead + N * PACK]
@@ -105,17 +105,21 @@ def tile_attend_x_sigmoid_cap_srt_kernel(tc, qT, kT, vT, vs, offs, out):
         nc.scalar.activation(q_grp[:], q_raw[:].rearrange("p j n -> p n j"), ACT.Copy)
         nc.vector.quantize_mx(out=q_codes[:].bitcast(FP8X4), scales=q_scales[:],
                               in_=q_grp[:].rearrange("p n j -> p (n j)"))
-        cast_keys(False, 0, 0, 576)
-        cast_keys(True, 0, 576, 768)
+        cast_keys(False, 0, 0, 512)
+        cast_keys(True, 0, 512, 768)
         cast_keys(True, 0, 768, T)
         gather_keys(0, 0, HALF)
         gather_keys(0, HALF, N)
         half_vs = sb.tile([P, PACK], F32, name="half_vs")
-        cast_keys(True, 1, 0, 288)
-        cast_keys(False, 1, 288, 768)
-        gather_keys(1, 0, HALF)
-        cast_keys(True, 2, 768, T)
-        gather_keys(1, HALF, N)
+        cast_keys(True, 1, 0, 256)
+        cast_keys(False, 1, 256, 640)
+        cast_keys(False, 1, 640, 768)
+        gather_keys(1, 0, 128)
+        gather_keys(1, 128, HALF)
+        cast_keys(True, 2, 768, 896)
+        cast_keys(False, 2, 896, T)
+        gather_keys(1, HALF, 384)
+        gather_keys(1, 384, N)
         join_keys(0, 0, PACK)
         for t in reversed(range(PACK)):
             join_keys(1, t, t + 1)

@@ -41,12 +41,13 @@ def tile_attend_x_sigmoid_cap_srt_kernel(tc, qT, kT, vT, vs, offs, out):
         pieces = [(0, 0, T), (1, 0, 768), (1, 768, T)]
         k_raw = []
         nc.scalar.dma_start(vs_pool[P - 1:P, :], vs[0:1, :])
-        nc.sync.dma_start(q_raw[:], qT[0].rearrange("(p j) n -> p j n", j=PACK))
         nc.sync.dma_start(offsets[:], offs)
         for i, (u, a, b) in enumerate(pieces):
             raw = sb.tile([P, 2, b - a], F32, name=f"k_raw{i}", tag=f"k_raw{i}", align_bytes=64)
             nc.sync.dma_start(raw[:], k_rows[:, u, :, a:b])
             k_raw.append(raw)
+            if i == 0:
+                nc.sync.dma_start(q_raw[:], qT[0].rearrange("(p j) n -> p j n", j=PACK))
         v_pool = [sb.tile([P, T], F32, name=f"v_pool{u}") for u in range(2)]
         for u in range(2):
             nc.sync.dma_start(v_pool[u][:], vT[u * P:(u + 1) * P, :])
@@ -102,14 +103,14 @@ def tile_attend_x_sigmoid_cap_srt_kernel(tc, qT, kT, vT, vs, offs, out):
         for t in range(PACK):
             nc.tensor.transpose(vs_ps[:, t, :], vs_g[:, t:N:PACK], ident[:])
 
-        nc.scalar.activation(q_grp[:], q_raw[:].rearrange("p j n -> p n j"), ACT.Copy)
-        nc.vector.quantize_mx(out=q_codes[:].bitcast(FP8X4), scales=q_scales[:],
-                              in_=q_grp[:].rearrange("p n j -> p (n j)"))
         cast_keys(False, 0, 0, 512)
         cast_keys(True, 0, 512, 768)
         cast_keys(True, 0, 768, T)
         gather_keys(0, 0, HALF)
         gather_keys(0, HALF, N)
+        nc.scalar.activation(q_grp[:], q_raw[:].rearrange("p j n -> p n j"), ACT.Copy)
+        nc.vector.quantize_mx(out=q_codes[:].bitcast(FP8X4), scales=q_scales[:],
+                              in_=q_grp[:].rearrange("p n j -> p (n j)"))
         half_vs = sb.tile([P, PACK], F32, name="half_vs")
         cast_keys(True, 1, 0, 256)
         cast_keys(False, 1, 256, 640)

@@ -30,8 +30,7 @@ def tile_attend_x_sigmoid_cap_srt_kernel(tc, qT, kT, vT, vs, offs, out):
 
         offsets = sb.tile([P, N // 16], U16, name="offsets")
         vs_pool = sb.tile([P, T], F32, name="vs_pool")
-        nc.gpsimd.memset(vs_pool[0:P - 1, 0:T // 2], 0.0)
-        nc.vector.memset(vs_pool[0:P - 1, T // 2:T], 0.0)
+        nc.vector.memset(vs_pool[0:P - 1, :], 0.0)
 
         ident = sb.tile([P, P], F32, name="ident")
         make_identity(nc, ident[:])
@@ -46,8 +45,7 @@ def tile_attend_x_sigmoid_cap_srt_kernel(tc, qT, kT, vT, vs, offs, out):
             raw = sb.tile([P, 2, b - a], F32, name=f"k_raw{i}", tag=f"k_raw{i}", align_bytes=64)
             nc.sync.dma_start(raw[:], k_rows[:, u, :, a:b])
             k_raw.append(raw)
-            if i == 0:
-                nc.sync.dma_start(q_raw[:], qT[0].rearrange("(p j) n -> p j n", j=PACK))
+        nc.sync.dma_start(q_raw[:], qT[0].rearrange("(p j) n -> p j n", j=PACK))
         v_pool = [sb.tile([P, T], F32, name=f"v_pool{u}") for u in range(2)]
         for u in range(2):
             nc.sync.dma_start(v_pool[u][:], vT[u * P:(u + 1) * P, :])
@@ -63,7 +61,7 @@ def tile_attend_x_sigmoid_cap_srt_kernel(tc, qT, kT, vT, vs, offs, out):
 
         k_pool = [sb.tile([P, 2 * T], BF16, name="k_pool0", align_bytes=64),
                   sb.tile([P, 2 * T], BF16, name="k_pool1", tag="k_raw0", align_bytes=64)]
-        SHARE = 384
+        SHARE = 128
         lead = HALF + SHARE // 2
         late = sb.tile([P, lead + N * PACK], BF16, name="late", align_bytes=64)
         k_grp = late[:, lead:lead + N * PACK]
@@ -102,16 +100,14 @@ def tile_attend_x_sigmoid_cap_srt_kernel(tc, qT, kT, vT, vs, offs, out):
         vs_ps = ps.tile([P, PACK, P], F32, name="vs_ps")
         for t in range(PACK):
             nc.tensor.transpose(vs_ps[:, t, :], vs_g[:, t:N:PACK], ident[:])
+        half_vs = sb.tile([P, PACK], F32, name="half_vs")
+        nc.scalar.activation(half_vs[:], vs_ps[:, :, P - 1], ACT.Copy, scale=0.5)
 
         cast_keys(False, 0, 0, 512)
         cast_keys(True, 0, 512, 768)
         cast_keys(True, 0, 768, T)
         gather_keys(0, 0, HALF)
         gather_keys(0, HALF, N)
-        nc.scalar.activation(q_grp[:], q_raw[:].rearrange("p j n -> p n j"), ACT.Copy)
-        nc.vector.quantize_mx(out=q_codes[:].bitcast(FP8X4), scales=q_scales[:],
-                              in_=q_grp[:].rearrange("p n j -> p (n j)"))
-        half_vs = sb.tile([P, PACK], F32, name="half_vs")
         cast_keys(True, 1, 0, 256)
         cast_keys(False, 1, 256, 640)
         cast_keys(False, 1, 640, 768)
@@ -121,12 +117,18 @@ def tile_attend_x_sigmoid_cap_srt_kernel(tc, qT, kT, vT, vs, offs, out):
         cast_keys(False, 2, 896, T)
         gather_keys(1, HALF, 384)
         gather_keys(1, 384, N)
+        for h in range(2):
+            cols = slice(h * NQ // 2, (h + 1) * NQ // 2)
+            nc.vector.tensor_copy(q_grp[:, cols, :], q_raw[:, :, cols].rearrange("p j n -> p n j"))
+        for h in range(2):
+            cols = slice(h * NQ // 2, (h + 1) * NQ // 2)
+            nc.vector.quantize_mx(out=q_codes[:, cols].bitcast(FP8X4), scales=q_scales[:, cols],
+                                  in_=q_grp[:, cols, :].rearrange("p n j -> p (n j)"))
         join_keys(0, 0, PACK)
         for t in reversed(range(PACK)):
             join_keys(1, t, t + 1)
         v_bf = sb.tile([P, T - N + SHARE], BF16, name="v_bf", tag="k_raw2", align_bytes=64)
-        nc.vector.tensor_copy(v_bf[:], v_pool[0][:, 0:T - N + SHARE])
-        nc.scalar.activation(half_vs[:], vs_ps[:, :, P - 1], ACT.Copy, scale=0.5)
+        nc.scalar.activation(v_bf[:], v_pool[0][:, 0:T - N + SHARE], ACT.Copy)
 
         score_ps = [ps.tile([P, 2, NQ], F32, name=f"score_ps{i}") for i in range(2)]
         for t in reversed(range(PACK)):

@@ -10,7 +10,6 @@ BYTES = 4 * (D * NQ + D * T + DV * T + T + NQ * DV) + 2 * 128 * (N // 16)
 F32 = mybir.dt.float32
 BF16 = mybir.dt.bfloat16
 U32 = mybir.dt.uint32
-I32 = mybir.dt.int32
 U16 = mybir.dt.uint16
 U8 = mybir.dt.uint8
 FP8X4 = mybir.dt.float8_e4m3fn_x4
@@ -19,7 +18,15 @@ ALU = mybir.AluOpType
 
 P = 128
 PACK = 4
+GROUP = 16
 HALF = N // 2
+QUARTER = N // 4
+SCALAR_TOKENS = 256
+SCALAR_SLOTS = 128
+
+
+def reach(slots):
+    return T - N + slots
 
 
 def tile_attend_x_sigmoid_cap_srt_kernel(tc, qT, kT, vT, vs, offs, out):
@@ -28,7 +35,7 @@ def tile_attend_x_sigmoid_cap_srt_kernel(tc, qT, kT, vT, vs, offs, out):
         sb = ctx.enter_context(tc.tile_pool(name="sb", bufs=1))
         ps = ctx.enter_context(tc.psum_pool(name="ps", bufs=1))
 
-        offsets = sb.tile([P, N // 16], U16, name="offsets")
+        offsets = sb.tile([P, N // GROUP], U16, name="offsets")
         vs_pool = sb.tile([P, T], F32, name="vs_pool")
         nc.vector.memset(vs_pool[0:P - 1, :], 0.0)
 
@@ -37,23 +44,18 @@ def tile_attend_x_sigmoid_cap_srt_kernel(tc, qT, kT, vT, vs, offs, out):
 
         q_raw = sb.tile([P, PACK, NQ], F32, name="q_raw")
         k_rows = kT.rearrange("(p u e) n -> p u e n", u=2, e=2)
-        pieces = [(0, 0, T), (1, 0, 768), (1, 768, T)]
+        key_loads = [(0, 0, T), (1, 0, reach(HALF)), (1, reach(HALF), T)]
         k_raw = []
         nc.scalar.dma_start(vs_pool[P - 1:P, :], vs[0:1, :])
         nc.sync.dma_start(offsets[:], offs)
-        for i, (u, a, b) in enumerate(pieces):
-            raw = sb.tile([P, 2, b - a], F32, name=f"k_raw{i}", tag=f"k_raw{i}", align_bytes=64)
-            nc.sync.dma_start(raw[:], k_rows[:, u, :, a:b])
+        for i, (u, first, end) in enumerate(key_loads):
+            raw = sb.tile([P, 2, end - first], F32, name=f"k_raw{i}", tag=f"k_raw{i}", align_bytes=64)
+            nc.sync.dma_start(raw[:], k_rows[:, u, :, first:end])
             k_raw.append(raw)
         nc.sync.dma_start(q_raw[:], qT[0].rearrange("(p j) n -> p j n", j=PACK))
-        v_pool = [sb.tile([P, T], F32, name=f"v_pool{u}") for u in range(2)]
-        for u in range(2):
-            nc.sync.dma_start(v_pool[u][:], vT[u * P:(u + 1) * P, :])
-
-        warm_in = sb.tile([P, 8], F32, name="warm_in")
-        warm = sb.tile([P, 8], F32, name="warm")
-        nc.vector.memset(warm_in[:], 0.0)
-        nc.scalar.activation(warm[:], warm_in[:], ACT.Tanh)
+        v_pool = [sb.tile([P, T], F32, name=f"v_pool{b}") for b in range(2)]
+        for b in range(2):
+            nc.sync.dma_start(v_pool[b][:], vT[b * P:(b + 1) * P, :])
 
         q_grp = sb.tile([P, NQ, PACK], BF16, name="q_grp", align_bytes=64)
         q_codes = sb.tile([P, NQ], U32, name="q_codes", align_bytes=64)
@@ -61,39 +63,36 @@ def tile_attend_x_sigmoid_cap_srt_kernel(tc, qT, kT, vT, vs, offs, out):
 
         k_pool = [sb.tile([P, 2 * T], BF16, name="k_pool0", align_bytes=64),
                   sb.tile([P, 2 * T], BF16, name="k_pool1", tag="k_raw0", align_bytes=64)]
-        SHARE = 128
-        lead = HALF + SHARE // 2
-        late = sb.tile([P, lead + N * PACK], BF16, name="late", align_bytes=64)
-        k_grp = late[:, lead:lead + N * PACK]
-        v_g = [late[:, 0:N], late[:, N:2 * N]]
+        lead = HALF + SCALAR_SLOTS // 2
+        shared = sb.tile([P, lead + N * PACK], BF16, name="shared", align_bytes=64)
+        k_grp = shared[:, lead:lead + N * PACK]
+        v_g = [shared[:, 0:N], shared[:, N:2 * N]]
         k_g = sb.tile([P, 2, 2 * N], BF16, name="k_g", align_bytes=64)
         k_codes = sb.tile([P, N], U32, name="k_codes", align_bytes=64)
         k_scales = sb.tile([P, N], U8, name="k_scales", align_bytes=64)
 
-        def cast_keys(on_scalar, i, n0, n1):
-            u, a, b = pieces[i]
-            pairs = k_pool[u][:].rearrange("p (n e) -> p n e", e=2)[:, n0:n1, :]
-            src = k_raw[i][:].rearrange("p e n -> p n e")[:, n0 - a:n1 - a, :]
-            if on_scalar:
-                nc.scalar.activation(pairs, src, ACT.Copy)
-            else:
-                nc.vector.tensor_copy(pairs, src)
+        def scalar_cast(dst, src):
+            nc.scalar.activation(dst, src, ACT.Copy)
+
+        def cast_keys(cast, load, n0, n1):
+            u, first, end = key_loads[load]
+            cast(k_pool[u][:].rearrange("p (n e) -> p n e", e=2)[:, n0:n1, :],
+                 k_raw[load][:].rearrange("p e n -> p n e")[:, n0 - first:n1 - first, :])
 
         def gather_keys(u, s0, s1):
-            window = k_pool[u][:].bitcast(U32)[:, 0:T - N + s1]
+            window = k_pool[u][:].bitcast(U32)[:, 0:reach(s1)]
             dst = k_g[:, u, :].bitcast(U32).rearrange("p (t m) -> p m t", t=PACK)
             nc.vector.tensor_copy(dst[:, s0 // PACK:s1 // PACK, :],
-                                  window.indirect(offsets[:, s0 // 16:s1 // 16]))
+                                  window.indirect(offsets[:, s0 // GROUP:s1 // GROUP]))
 
         def join_keys(h, t0, t1):
             src = k_g[:].bitcast(U32).rearrange("p u (t m) -> p t m u", t=PACK)
             dst = k_grp.bitcast(U32).rearrange("p (t m u) -> p t m u", t=PACK, u=2)
-            half = slice(h * P // 2, (h + 1) * P // 2)
-            nc.scalar.copy(dst[:, t0:t1, half, :], src[:, t0:t1, half, :])
+            columns = slice(h * P // 2, (h + 1) * P // 2)
+            nc.scalar.copy(dst[:, t0:t1, columns, :], src[:, t0:t1, columns, :])
 
-        def slot_pairs(u, s0, s1):
-            return v_g[u].rearrange("p (w m s) -> p m w s", w=2, s=2)[:, s0 // PACK:s1 // PACK, :, :]
-
+        def value_words(b, s0, s1):
+            return v_g[b].rearrange("p (w m s) -> p m w s", w=2, s=2)[:, s0 // PACK:s1 // PACK, :, :]
 
         vs_g = sb.tile([P, N], F32, name="vs_g")
         nc.vector.tensor_copy(vs_g[:], vs_pool[:].indirect(offsets[:]))
@@ -103,32 +102,34 @@ def tile_attend_x_sigmoid_cap_srt_kernel(tc, qT, kT, vT, vs, offs, out):
         half_vs = sb.tile([P, PACK], F32, name="half_vs")
         nc.scalar.activation(half_vs[:], vs_ps[:, :, P - 1], ACT.Copy, scale=0.5)
 
-        cast_keys(False, 0, 0, 512)
-        cast_keys(True, 0, 512, 768)
-        cast_keys(True, 0, 768, T)
+        cast_keys(nc.vector.tensor_copy, 0, 0, reach(0))
+        cast_keys(scalar_cast, 0, reach(0), reach(HALF))
+        cast_keys(scalar_cast, 0, reach(HALF), T)
         gather_keys(0, 0, HALF)
         gather_keys(0, HALF, N)
-        cast_keys(True, 1, 0, 256)
-        cast_keys(False, 1, 256, 640)
-        cast_keys(False, 1, 640, 768)
-        gather_keys(1, 0, 128)
-        gather_keys(1, 128, HALF)
-        cast_keys(True, 2, 768, 896)
-        cast_keys(False, 2, 896, T)
-        gather_keys(1, HALF, 384)
-        gather_keys(1, 384, N)
-        for h in range(2):
-            cols = slice(h * NQ // 2, (h + 1) * NQ // 2)
+
+        cast_keys(scalar_cast, 1, 0, SCALAR_TOKENS)
+        cast_keys(nc.vector.tensor_copy, 1, SCALAR_TOKENS, reach(QUARTER))
+        cast_keys(nc.vector.tensor_copy, 1, reach(QUARTER), reach(HALF))
+        gather_keys(1, 0, QUARTER)
+        gather_keys(1, QUARTER, HALF)
+        cast_keys(scalar_cast, 2, reach(HALF), reach(HALF + QUARTER))
+        cast_keys(nc.vector.tensor_copy, 2, reach(HALF + QUARTER), T)
+        gather_keys(1, HALF, HALF + QUARTER)
+        gather_keys(1, HALF + QUARTER, N)
+
+        query_halves = [slice(0, NQ // 2), slice(NQ // 2, NQ)]
+        for cols in query_halves:
             nc.vector.tensor_copy(q_grp[:, cols, :], q_raw[:, :, cols].rearrange("p j n -> p n j"))
-        for h in range(2):
-            cols = slice(h * NQ // 2, (h + 1) * NQ // 2)
+        for cols in query_halves:
             nc.vector.quantize_mx(out=q_codes[:, cols].bitcast(FP8X4), scales=q_scales[:, cols],
                                   in_=q_grp[:, cols, :].rearrange("p n j -> p (n j)"))
+
         join_keys(0, 0, PACK)
         for t in reversed(range(PACK)):
             join_keys(1, t, t + 1)
-        v_bf = sb.tile([P, T - N + SHARE], BF16, name="v_bf", tag="k_raw2", align_bytes=64)
-        nc.scalar.activation(v_bf[:], v_pool[0][:, 0:T - N + SHARE], ACT.Copy)
+        v_bf = sb.tile([P, reach(SCALAR_SLOTS)], BF16, name="v_bf", tag="k_raw2", align_bytes=64)
+        scalar_cast(v_bf[:], v_pool[0][:, 0:reach(SCALAR_SLOTS)])
 
         score_ps = [ps.tile([P, 2, NQ], F32, name=f"score_ps{i}") for i in range(2)]
         for t in reversed(range(PACK)):
@@ -141,74 +142,60 @@ def tile_attend_x_sigmoid_cap_srt_kernel(tc, qT, kT, vT, vs, offs, out):
                                 lhsT_scale=k_scales[:, cols], rhs=q_codes[:].bitcast(FP8X4),
                                 rhs_scale=q_scales[:], start=True, stop=True)
 
-        v_ps = [ps.tile([P, 2, P], F32, name=f"v_ps{u}") for u in range(2)]
-        v_grp = [sb.tile([P, P * PACK], BF16, name=f"v_grp{u}", align_bytes=64) for u in range(2)]
-        v_scales = [sb.tile([P, P], U8, name=f"v_scales{u}", align_bytes=64) for u in range(2)]
+        v_ps = [ps.tile([P, 2, P], F32, name=f"v_ps{b}") for b in range(2)]
+        v_scales = [sb.tile([P, P], U8, name=f"v_scales{b}", align_bytes=64) for b in range(2)]
+        v_codes = [sb.tile([P, P], U32, name=f"v_codes{b}", align_bytes=64) for b in range(2)]
+        v_grp = [sb.tile([P, P * PACK], BF16, name=f"v_grp{b}", align_bytes=64) for b in range(2)]
 
-        def turn_values(u):
-            words = v_g[u].bitcast(F32)
+        def turn_values(b):
+            words = v_g[b].bitcast(F32)
             for w in range(2):
-                nc.tensor.transpose(v_ps[u][:, w, :], words[:, w * P:(w + 1) * P], ident[:])
+                nc.tensor.transpose(v_ps[b][:, w, :], words[:, w * P:(w + 1) * P], ident[:])
 
-        nc.scalar.activation(slot_pairs(0, 0, SHARE), v_bf[:].indirect(offsets[:, 0:SHARE // 16]), ACT.Copy)
-        nc.vector.tensor_copy(slot_pairs(0, SHARE, N), v_pool[0][:].indirect(offsets[:, SHARE // 16:N // 16]))
+        scalar_cast(value_words(0, 0, SCALAR_SLOTS), v_bf[:].indirect(offsets[:, 0:SCALAR_SLOTS // GROUP]))
+        nc.vector.tensor_copy(value_words(0, SCALAR_SLOTS, N),
+                              v_pool[0][:].indirect(offsets[:, SCALAR_SLOTS // GROUP:N // GROUP]))
         turn_values(0)
-        nc.vector.tensor_copy(slot_pairs(1, 0, N), v_pool[1][:].indirect(offsets[:]))
+        nc.vector.tensor_copy(value_words(1, 0, N), v_pool[1][:].indirect(offsets[:]))
         turn_values(1)
 
-        def pack_values(copy, u):
-            copy(v_grp[u][:].bitcast(F32).rearrange("p (e w) -> p e w", w=2),
-                 v_ps[u][:].rearrange("p w e -> p e w"))
-
-        def quantize_values(u):
-            nc.vector.quantize_mx(out=v_codes[u][:].bitcast(FP8X4), scales=v_scales[u][:], in_=v_grp[u][:])
-
-        pack_values(nc.vector.tensor_copy, 0)
-
-        QH = NQ // 2
-        capped = sb.tile([P, 2, NQ, 2], F32, name="capped", tag="capped", align_bytes=64)
-        QQ = NQ // 4
-        centred = [sb.tile([P, QQ, PACK], F32, name=f"centred{c}") for c in range(4)]
-        v_codes = [sb.tile([P, P], U32, name="v_codes0", tag="capped", align_bytes=64),
-                   sb.tile([P, P], U32, name="v_codes1", align_bytes=64)]
+        quarter_q = NQ // 4
+        capped = sb.tile([P, 2, NQ, 2], F32, name="capped")
+        centred = [sb.tile([P, quarter_q, PACK], F32, name=f"centred{c}") for c in range(4)]
         w_grp = sb.tile([P, NQ, PACK], BF16, name="w_grp", align_bytes=64)
         w_codes = sb.tile([P, NQ], U32, name="w_codes", align_bytes=64)
         w_scales = sb.tile([P, NQ], U8, name="w_scales", align_bytes=64)
 
-        def cap(i, q0, q1):
-            nc.scalar.activation(capped[:, i, q0:q1, :], score_ps[i][:, :, q0:q1].rearrange("p s n -> p n s"),
+        def cap(i, cols):
+            nc.scalar.activation(capped[:, i, cols, :], score_ps[i][:, :, cols].rearrange("p s n -> p n s"),
                                  ACT.Tanh, scale=0.5)
 
-        cap(1, 0, NQ)
-        cap(0, 0, QH)
-        cap(0, QH, NQ)
+        cap(1, slice(0, NQ))
+        for cols in query_halves:
+            cap(0, cols)
         for c in range(4):
+            cols = slice(c * quarter_q, (c + 1) * quarter_q)
             nc.scalar.activation(centred[c][:].rearrange("p n (i s) -> p n i s", i=2),
-                                 capped[:, :, c * QQ:(c + 1) * QQ, :].rearrange("p i n s -> p n i s"), ACT.Tanh)
-        pack_values(nc.scalar.copy, 1)
-
-        def weigh(c):
-            nc.vector.scalar_tensor_tensor(w_grp[:, c * QQ:(c + 1) * QQ, :], centred[c][:], 1.0,
-                                           half_vs[:].unsqueeze(1).to_broadcast([P, QQ, PACK]),
+                                 capped[:, :, cols, :].rearrange("p i n s -> p n i s"), ACT.Tanh)
+        for b in range(2):
+            nc.scalar.copy(v_grp[b][:].bitcast(F32).rearrange("p (e w) -> p e w", w=2),
+                           v_ps[b][:].rearrange("p w e -> p e w"))
+        for c in range(4):
+            cols = slice(c * quarter_q, (c + 1) * quarter_q)
+            nc.vector.scalar_tensor_tensor(w_grp[:, cols, :], centred[c][:], 1.0,
+                                           half_vs[:].unsqueeze(1).to_broadcast([P, quarter_q, PACK]),
                                            ALU.add, ALU.mult)
-
-        def quantize_weights(h):
-            cols = slice(h * QH, (h + 1) * QH)
+        for cols in query_halves:
             nc.vector.quantize_mx(out=w_codes[:, cols].bitcast(FP8X4), scales=w_scales[:, cols],
                                   in_=w_grp[:, cols, :].rearrange("p n t -> p (n t)"))
+        for b in range(2):
+            nc.vector.quantize_mx(out=v_codes[b][:].bitcast(FP8X4), scales=v_scales[b][:], in_=v_grp[b][:])
 
-        for c in range(4):
-            weigh(c)
-        quantize_weights(0)
-        quantize_values(0)
-        quantize_weights(1)
-        quantize_values(1)
-
-        y_ps = [ps.tile([P, P], F32, name=f"y_ps{u}") for u in range(2)]
+        y_ps = [ps.tile([P, P], F32, name=f"y_ps{b}") for b in range(2)]
         y = sb.tile([P, DV], F32, name="y")
-        for u in range(2):
-            nc.tensor.matmul_mx(out=y_ps[u][:], lhsT=w_codes[:].bitcast(FP8X4), lhsT_scale=w_scales[:],
-                                rhs=v_codes[u][:].bitcast(FP8X4), rhs_scale=v_scales[u][:],
+        for b in range(2):
+            nc.tensor.matmul_mx(out=y_ps[b][:], lhsT=w_codes[:].bitcast(FP8X4), lhsT_scale=w_scales[:],
+                                rhs=v_codes[b][:].bitcast(FP8X4), rhs_scale=v_scales[b][:],
                                 start=True, stop=True)
         nc.vector.tensor_scalar(y[:, 0:P], y_ps[0][:], 1.0 / 16.0, None, ALU.mult)
         nc.scalar.activation(y[:, P:DV], y_ps[1][:], ACT.Copy, scale=1.0 / 16.0)

@@ -57,6 +57,11 @@ def tile_attend_x_sigmoid_cap_srt_kernel(tc, qT, kT, vT, vs, offs, out):
         for b in range(2):
             nc.sync.dma_start(v_pool[b][:], vT[b * P:(b + 1) * P, :])
 
+        warm_in = sb.tile([P, 8], F32, name="warm_in")
+        warm = sb.tile([P, 8], F32, name="warm")
+        nc.vector.memset(warm_in[:], 0.0)
+        nc.scalar.activation(warm[:], warm_in[:], ACT.Tanh)
+
         q_grp = sb.tile([P, NQ, PACK], BF16, name="q_grp", align_bytes=64)
         q_codes = sb.tile([P, NQ], U32, name="q_codes", align_bytes=64)
         q_scales = sb.tile([P, NQ], U8, name="q_scales", align_bytes=64)

@@ -21,7 +21,8 @@ PACK = 4
 GROUP = 16
 HALF = N // 2
 QUARTER = N // 4
-SCALAR_TOKENS = 256
+SCALAR_TOKENS = 192
+EARLY = T // 2
 SCALAR_SLOTS = 128
 
 
@@ -43,15 +44,13 @@ def tile_attend_x_sigmoid_cap_srt_kernel(tc, qT, kT, vT, vs, offs, out):
         make_identity(nc, ident[:])
 
         q_raw = sb.tile([P, PACK, NQ], F32, name="q_raw")
-        k_rows = kT.rearrange("(p u e) n -> p u e n", u=2, e=2)
-        key_loads = [(0, 0, T), (1, 0, reach(HALF)), (1, reach(HALF), T)]
-        k_raw = []
+        k_rows = kT.rearrange("(p u e) n -> p u (e n)", u=2, e=2)
+        k_raw = [sb.tile([P, 2 * T], F32, name=f"k_raw{u}", tag=f"k_raw{u}", align_bytes=64) for u in range(2)]
         nc.scalar.dma_start(vs_pool[P - 1:P, :], vs[0:1, :])
         nc.sync.dma_start(offsets[:], offs)
-        for i, (u, first, end) in enumerate(key_loads):
-            raw = sb.tile([P, 2, end - first], F32, name=f"k_raw{i}", tag=f"k_raw{i}", align_bytes=64)
-            nc.sync.dma_start(raw[:], k_rows[:, u, :, first:end])
-            k_raw.append(raw)
+        for u, first, end in [(0, 0, T + EARLY), (0, T + EARLY, 2 * T),
+                              (1, 0, T + EARLY), (1, T + EARLY, T + reach(HALF)), (1, T + reach(HALF), 2 * T)]:
+            nc.sync.dma_start(k_raw[u][:, first:end], k_rows[:, u, first:end])
         nc.sync.dma_start(q_raw[:], qT[0].rearrange("(p j) n -> p j n", j=PACK))
         v_pool = [sb.tile([P, T], F32, name=f"v_pool{b}") for b in range(2)]
         for b in range(2):
@@ -62,7 +61,7 @@ def tile_attend_x_sigmoid_cap_srt_kernel(tc, qT, kT, vT, vs, offs, out):
         nc.vector.memset(warm_in[:], 0.0)
         nc.scalar.activation(warm[:], warm_in[:], ACT.Tanh)
 
-        q_grp = sb.tile([P, NQ, PACK], BF16, name="q_grp", align_bytes=64)
+        q_grp = sb.tile([P, NQ, PACK], BF16, name="q_grp", tag="k_raw1", align_bytes=64)
         q_codes = sb.tile([P, NQ], U32, name="q_codes", align_bytes=64)
         q_scales = sb.tile([P, NQ], U8, name="q_scales", align_bytes=64)
 
@@ -79,10 +78,9 @@ def tile_attend_x_sigmoid_cap_srt_kernel(tc, qT, kT, vT, vs, offs, out):
         def scalar_cast(dst, src):
             nc.scalar.activation(dst, src, ACT.Copy)
 
-        def cast_keys(cast, load, n0, n1):
-            u, first, end = key_loads[load]
+        def cast_keys(cast, u, n0, n1):
             cast(k_pool[u][:].rearrange("p (n e) -> p n e", e=2)[:, n0:n1, :],
-                 k_raw[load][:].rearrange("p e n -> p n e")[:, n0 - first:n1 - first, :])
+                 k_raw[u][:].rearrange("p (e n) -> p n e", e=2)[:, n0:n1, :])
 
         def gather_keys(u, s0, s1):
             window = k_pool[u][:].bitcast(U32)[:, 0:reach(s1)]
@@ -90,10 +88,10 @@ def tile_attend_x_sigmoid_cap_srt_kernel(tc, qT, kT, vT, vs, offs, out):
             nc.vector.tensor_copy(dst[:, s0 // PACK:s1 // PACK, :],
                                   window.indirect(offsets[:, s0 // GROUP:s1 // GROUP]))
 
-        def join_keys(h, t0, t1):
+        def join_keys(s0, s1, t0, t1):
             src = k_g[:].bitcast(U32).rearrange("p u (t m) -> p t m u", t=PACK)
             dst = k_grp.bitcast(U32).rearrange("p (t m u) -> p t m u", t=PACK, u=2)
-            columns = slice(h * P // 2, (h + 1) * P // 2)
+            columns = slice(s0 // PACK, s1 // PACK)
             nc.scalar.copy(dst[:, t0:t1, columns, :], src[:, t0:t1, columns, :])
 
         def value_words(b, s0, s1):
@@ -107,21 +105,15 @@ def tile_attend_x_sigmoid_cap_srt_kernel(tc, qT, kT, vT, vs, offs, out):
         half_vs = sb.tile([P, PACK], F32, name="half_vs")
         nc.scalar.activation(half_vs[:], vs_ps[:, :, P - 1], ACT.Copy, scale=0.5)
 
-        cast_keys(nc.vector.tensor_copy, 0, 0, reach(0))
-        cast_keys(scalar_cast, 0, reach(0), reach(HALF))
-        cast_keys(scalar_cast, 0, reach(HALF), T)
-        gather_keys(0, 0, HALF)
-        gather_keys(0, HALF, N)
-
-        cast_keys(scalar_cast, 1, 0, SCALAR_TOKENS)
-        cast_keys(nc.vector.tensor_copy, 1, SCALAR_TOKENS, reach(QUARTER))
-        cast_keys(nc.vector.tensor_copy, 1, reach(QUARTER), reach(HALF))
-        gather_keys(1, 0, QUARTER)
-        gather_keys(1, QUARTER, HALF)
-        cast_keys(scalar_cast, 2, reach(HALF), reach(HALF + QUARTER))
-        cast_keys(nc.vector.tensor_copy, 2, reach(HALF + QUARTER), T)
-        gather_keys(1, HALF, HALF + QUARTER)
-        gather_keys(1, HALF + QUARTER, N)
+        for u in range(2):
+            cast_keys(scalar_cast, u, 0, SCALAR_TOKENS)
+            cast_keys(nc.vector.tensor_copy, u, SCALAR_TOKENS, EARLY)
+            cast_keys(nc.vector.tensor_copy, u, EARLY, reach(QUARTER))
+            cast_keys(nc.vector.tensor_copy, u, reach(QUARTER), reach(HALF))
+            cast_keys(scalar_cast, u, reach(HALF), reach(HALF + QUARTER))
+            cast_keys(scalar_cast, u, reach(HALF + QUARTER), T)
+            for s0 in range(0, N, QUARTER):
+                gather_keys(u, s0, s0 + QUARTER)
 
         query_halves = [slice(0, NQ // 2), slice(NQ // 2, NQ)]
         for cols in query_halves:
@@ -130,10 +122,11 @@ def tile_attend_x_sigmoid_cap_srt_kernel(tc, qT, kT, vT, vs, offs, out):
             nc.vector.quantize_mx(out=q_codes[:, cols].bitcast(FP8X4), scales=q_scales[:, cols],
                                   in_=q_grp[:, cols, :].rearrange("p n j -> p (n j)"))
 
-        join_keys(0, 0, PACK)
-        for t in reversed(range(PACK)):
-            join_keys(1, t, t + 1)
-        v_bf = sb.tile([P, reach(SCALAR_SLOTS)], BF16, name="v_bf", tag="k_raw2", align_bytes=64)
+        for s0 in range(0, N - QUARTER, QUARTER):
+            join_keys(s0, s0 + QUARTER, 0, PACK)
+        for t0 in (2, 0):
+            join_keys(N - QUARTER, N, t0, t0 + 2)
+        v_bf = sb.tile([P, reach(SCALAR_SLOTS)], BF16, name="v_bf", tag="k_raw1", align_bytes=64)
         scalar_cast(v_bf[:], v_pool[0][:, 0:reach(SCALAR_SLOTS)])
 
         score_ps = [ps.tile([P, 2, NQ], F32, name=f"score_ps{i}") for i in range(2)]

@@ -84,8 +84,8 @@ def tile_attend_x_sigmoid_cap_srt_kernel(tc, qT, kT, vT, vs, offs, out):
 
         def gather_keys(u, s0, s1):
             window = k_pool[u][:].bitcast(U32)[:, 0:reach(s1)]
-            dst = k_g[:, u, :].bitcast(U32).rearrange("p (t m) -> p m t", t=PACK)
-            nc.vector.tensor_copy(dst[:, s0 // PACK:s1 // PACK, :],
+            dst = k_g[:, u, :].bitcast(U32).rearrange("p (w s g r) -> p g w r s", w=2, s=2, r=8)
+            nc.vector.tensor_copy(dst[:, s0 // 32:s1 // 32, :, :, :],
                                   window.indirect(offsets[:, s0 // GROUP:s1 // GROUP]))
 
         def join_keys(s0, s1, t0, t1):
@@ -95,13 +95,14 @@ def tile_attend_x_sigmoid_cap_srt_kernel(tc, qT, kT, vT, vs, offs, out):
             nc.scalar.copy(dst[:, t0:t1, columns, :], src[:, t0:t1, columns, :])
 
         def value_words(b, s0, s1):
-            return v_g[b].rearrange("p (w m s) -> p m w s", w=2, s=2)[:, s0 // PACK:s1 // PACK, :, :]
+            return v_g[b].rearrange("p (w g x) -> p g w x", w=2, x=16)[:, s0 // 32:s1 // 32, :, :]
 
         vs_g = sb.tile([P, N], F32, name="vs_g")
-        nc.vector.tensor_copy(vs_g[:], vs_pool[:].indirect(offsets[:]))
+        nc.vector.tensor_copy(vs_g[:].bitcast(U32).rearrange("p (w s g r) -> p g w r s", w=2, s=2, r=8),
+                              vs_pool[:].bitcast(U32).indirect(offsets[:]))
         vs_ps = ps.tile([P, PACK, P], F32, name="vs_ps")
         for t in range(PACK):
-            nc.tensor.transpose(vs_ps[:, t, :], vs_g[:, t:N:PACK], ident[:])
+            nc.tensor.transpose(vs_ps[:, t, :], vs_g[:, t * P:(t + 1) * P], ident[:])
         half_vs = sb.tile([P, PACK], F32, name="half_vs")
         nc.scalar.activation(half_vs[:], vs_ps[:, :, P - 1], ACT.Copy, scale=0.5)
 

@@ -23,7 +23,7 @@ HALF = N // 2
 QUARTER = N // 4
 SCALAR_TOKENS = 192
 EARLY = T // 2
-SCALAR_SLOTS = 128
+SCALAR_SLOTS = 320
 
 
 def reach(slots):
@@ -44,13 +44,13 @@ def tile_attend_x_sigmoid_cap_srt_kernel(tc, qT, kT, vT, vs, offs, out):
         make_identity(nc, ident[:])
 
         q_raw = sb.tile([P, PACK, NQ], F32, name="q_raw")
-        k_rows = kT.rearrange("(p u e) n -> p u (e n)", u=2, e=2)
+        k_rows = kT.rearrange("(p u e) n -> p u e n", u=2, e=2)
         k_raw = [sb.tile([P, 2 * T], F32, name=f"k_raw{u}", tag=f"k_raw{u}", align_bytes=64) for u in range(2)]
         nc.scalar.dma_start(vs_pool[P - 1:P, :], vs[0:1, :])
         nc.sync.dma_start(offsets[:], offs)
-        for u, first, end in [(0, 0, T + EARLY), (0, T + EARLY, 2 * T),
-                              (1, 0, T + EARLY), (1, T + EARLY, T + reach(HALF)), (1, T + reach(HALF), 2 * T)]:
-            nc.sync.dma_start(k_raw[u][:, first:end], k_rows[:, u, first:end])
+        for u, first, end in [(0, 0, reach(HALF)), (0, reach(HALF), T),
+                              (1, 0, EARLY), (1, EARLY, reach(HALF)), (1, reach(HALF), T)]:
+            nc.sync.dma_start(k_raw[u][:].rearrange("p (e n) -> p e n", e=2)[:, :, first:end], k_rows[:, u, :, first:end])
         nc.sync.dma_start(q_raw[:], qT[0].rearrange("(p j) n -> p j n", j=PACK))
         v_pool = [sb.tile([P, T], F32, name=f"v_pool{b}") for b in range(2)]
         for b in range(2):
@@ -67,7 +67,7 @@ def tile_attend_x_sigmoid_cap_srt_kernel(tc, qT, kT, vT, vs, offs, out):
 
         k_pool = [sb.tile([P, 2 * T], BF16, name="k_pool0", align_bytes=64),
                   sb.tile([P, 2 * T], BF16, name="k_pool1", tag="k_raw0", align_bytes=64)]
-        lead = HALF + SCALAR_SLOTS // 2
+        lead = SCALAR_SLOTS
         shared = sb.tile([P, lead + N * PACK], BF16, name="shared", align_bytes=64)
         k_grp = shared[:, lead:lead + N * PACK]
         v_g = [shared[:, 0:N], shared[:, N:2 * N]]
@@ -84,8 +84,8 @@ def tile_attend_x_sigmoid_cap_srt_kernel(tc, qT, kT, vT, vs, offs, out):
 
         def gather_keys(u, s0, s1):
             window = k_pool[u][:].bitcast(U32)[:, 0:reach(s1)]
-            dst = k_g[:, u, :].bitcast(U32).rearrange("p (w s g r) -> p g w r s", w=2, s=2, r=8)
-            nc.vector.tensor_copy(dst[:, s0 // 32:s1 // 32, :, :, :],
+            dst = k_g[:, u, :].bitcast(U32).rearrange("p (t m) -> p m t", t=PACK)
+            nc.vector.tensor_copy(dst[:, s0 // PACK:s1 // PACK, :],
                                   window.indirect(offsets[:, s0 // GROUP:s1 // GROUP]))
 
         def join_keys(s0, s1, t0, t1):
@@ -94,27 +94,28 @@ def tile_attend_x_sigmoid_cap_srt_kernel(tc, qT, kT, vT, vs, offs, out):
             columns = slice(s0 // PACK, s1 // PACK)
             nc.scalar.copy(dst[:, t0:t1, columns, :], src[:, t0:t1, columns, :])
 
-        def value_words(b, s0, s1):
-            return v_g[b].rearrange("p (w g x) -> p g w x", w=2, x=16)[:, s0 // 32:s1 // 32, :, :]
-
         vs_g = sb.tile([P, N], F32, name="vs_g")
-        nc.vector.tensor_copy(vs_g[:].bitcast(U32).rearrange("p (w s g r) -> p g w r s", w=2, s=2, r=8),
+        nc.vector.tensor_copy(vs_g[:].bitcast(U32).rearrange("p (t m) -> p m t", t=PACK),
                               vs_pool[:].bitcast(U32).indirect(offsets[:]))
         vs_ps = ps.tile([P, PACK, P], F32, name="vs_ps")
         for t in range(PACK):
             nc.tensor.transpose(vs_ps[:, t, :], vs_g[:, t * P:(t + 1) * P], ident[:])
-        half_vs = sb.tile([P, PACK], F32, name="half_vs")
-        nc.scalar.activation(half_vs[:], vs_ps[:, :, P - 1], ACT.Copy, scale=0.5)
 
-        for u in range(2):
-            cast_keys(scalar_cast, u, 0, SCALAR_TOKENS)
-            cast_keys(nc.vector.tensor_copy, u, SCALAR_TOKENS, EARLY)
-            cast_keys(nc.vector.tensor_copy, u, EARLY, reach(QUARTER))
-            cast_keys(nc.vector.tensor_copy, u, reach(QUARTER), reach(HALF))
-            cast_keys(scalar_cast, u, reach(HALF), reach(HALF + QUARTER))
-            cast_keys(scalar_cast, u, reach(HALF + QUARTER), T)
-            for s0 in range(0, N, QUARTER):
-                gather_keys(u, s0, s0 + QUARTER)
+        cast_keys(scalar_cast, 0, 0, 256)
+        cast_keys(nc.vector.tensor_copy, 0, 256, reach(QUARTER))
+        cast_keys(nc.vector.tensor_copy, 0, reach(QUARTER), reach(HALF))
+        cast_keys(scalar_cast, 0, reach(HALF), T)
+        gather_keys(0, 0, QUARTER)
+        gather_keys(0, QUARTER, HALF)
+        gather_keys(0, HALF, N)
+        cast_keys(scalar_cast, 1, 0, 384)
+        cast_keys(nc.vector.tensor_copy, 1, 384, EARLY)
+        cast_keys(nc.vector.tensor_copy, 1, EARLY, reach(QUARTER))
+        cast_keys(nc.vector.tensor_copy, 1, reach(QUARTER), reach(HALF))
+        cast_keys(scalar_cast, 1, reach(HALF), reach(HALF + QUARTER))
+        cast_keys(scalar_cast, 1, reach(HALF + QUARTER), T)
+        for s0 in range(0, N, QUARTER):
+            gather_keys(1, s0, s0 + QUARTER)
 
         query_halves = [slice(0, NQ // 2), slice(NQ // 2, NQ)]
         for cols in query_halves:
@@ -127,8 +128,6 @@ def tile_attend_x_sigmoid_cap_srt_kernel(tc, qT, kT, vT, vs, offs, out):
             join_keys(s0, s0 + QUARTER, 0, PACK)
         for t0 in (2, 0):
             join_keys(N - QUARTER, N, t0, t0 + 2)
-        v_bf = sb.tile([P, reach(SCALAR_SLOTS)], BF16, name="v_bf", tag="k_raw1", align_bytes=64)
-        scalar_cast(v_bf[:], v_pool[0][:, 0:reach(SCALAR_SLOTS)])
 
         score_ps = [ps.tile([P, 2, NQ], F32, name=f"score_ps{i}") for i in range(2)]
         for t in reversed(range(PACK)):
@@ -149,13 +148,13 @@ def tile_attend_x_sigmoid_cap_srt_kernel(tc, qT, kT, vT, vs, offs, out):
         def turn_values(b):
             words = v_g[b].bitcast(F32)
             for w in range(2):
-                nc.tensor.transpose(v_ps[b][:, w, :], words[:, w * P:(w + 1) * P], ident[:])
+                nc.tensor.transpose(v_ps[b][:, w, :], words[:, w:2 * P:2], ident[:])
 
-        scalar_cast(value_words(0, 0, SCALAR_SLOTS), v_bf[:].indirect(offsets[:, 0:SCALAR_SLOTS // GROUP]))
-        nc.vector.tensor_copy(value_words(0, SCALAR_SLOTS, N),
+        scalar_cast(v_g[0][:, 0:SCALAR_SLOTS], v_pool[0][:].indirect(offsets[:, 0:SCALAR_SLOTS // GROUP]))
+        nc.vector.tensor_copy(v_g[0][:, SCALAR_SLOTS:N],
                               v_pool[0][:].indirect(offsets[:, SCALAR_SLOTS // GROUP:N // GROUP]))
         turn_values(0)
-        nc.vector.tensor_copy(value_words(1, 0, N), v_pool[1][:].indirect(offsets[:]))
+        nc.vector.tensor_copy(v_g[1], v_pool[1][:].indirect(offsets[:]))
         turn_values(1)
 
         quarter_q = NQ // 4
@@ -182,7 +181,7 @@ def tile_attend_x_sigmoid_cap_srt_kernel(tc, qT, kT, vT, vs, offs, out):
         for c in range(4):
             cols = slice(c * quarter_q, (c + 1) * quarter_q)
             nc.vector.scalar_tensor_tensor(w_grp[:, cols, :], centred[c][:], 1.0,
-                                           half_vs[:].unsqueeze(1).to_broadcast([P, quarter_q, PACK]),
+                                           vs_ps[:, :, P - 1].unsqueeze(1).to_broadcast([P, quarter_q, PACK]),
                                            ALU.add, ALU.mult)
         for cols in query_halves:
             nc.vector.quantize_mx(out=w_codes[:, cols].bitcast(FP8X4), scales=w_scales[:, cols],
@@ -196,7 +195,7 @@ def tile_attend_x_sigmoid_cap_srt_kernel(tc, qT, kT, vT, vs, offs, out):
             nc.tensor.matmul_mx(out=y_ps[b][:], lhsT=w_codes[:].bitcast(FP8X4), lhsT_scale=w_scales[:],
                                 rhs=v_codes[b][:].bitcast(FP8X4), rhs_scale=v_scales[b][:],
                                 start=True, stop=True)
-        nc.vector.tensor_scalar(y[:, 0:P], y_ps[0][:], 1.0 / 16.0, None, ALU.mult)
-        nc.scalar.activation(y[:, P:DV], y_ps[1][:], ACT.Copy, scale=1.0 / 16.0)
+        nc.vector.tensor_scalar(y[:, 0:P], y_ps[0][:], 1.0 / 32.0, None, ALU.mult)
+        nc.scalar.activation(y[:, P:DV], y_ps[1][:], ACT.Copy, scale=1.0 / 32.0)
         nc.sync.dma_start(out[0, :, 0:P], y[:, 0:P])
         nc.scalar.dma_start(out[0, :, P:DV], y[:, P:DV])

@@ -24,6 +24,7 @@ QUARTER = N // 4
 SCALAR_TOKENS = 192
 EARLY = T // 2
 SCALAR_SLOTS = 320
+LAST_CUTS = [0, 128, 320, 512]
 
 
 def reach(slots):
@@ -34,6 +35,7 @@ def tile_attend_x_sigmoid_cap_srt_kernel(tc, qT, kT, vT, vs, offs, out):
     nc = tc.nc
     with ExitStack() as ctx:
         sb = ctx.enter_context(tc.tile_pool(name="sb", bufs=1))
+        reuse = ctx.enter_context(tc.tile_pool(name="reuse", bufs=1))
         ps = ctx.enter_context(tc.psum_pool(name="ps", bufs=1))
 
         offsets = sb.tile([P, N // GROUP], U16, name="offsets")
@@ -49,26 +51,28 @@ def tile_attend_x_sigmoid_cap_srt_kernel(tc, qT, kT, vT, vs, offs, out):
         nc.scalar.dma_start(vs_pool[P - 1:P, :], vs[0:1, :])
         nc.sync.dma_start(offsets[:], offs)
         for u, first, end in [(0, 0, reach(HALF)), (0, reach(HALF), T),
-                              (1, 0, EARLY), (1, EARLY, reach(HALF)), (1, reach(HALF), T)]:
+                              (1, 0, reach(QUARTER)), (1, reach(QUARTER), reach(N - QUARTER)),
+                              (1, reach(N - QUARTER), T)]:
             nc.sync.dma_start(k_raw[u][:].rearrange("p (e n) -> p e n", e=2)[:, :, first:end], k_rows[:, u, :, first:end])
         nc.sync.dma_start(q_raw[:], qT[0].rearrange("(p j) n -> p j n", j=PACK))
-        v_pool = [sb.tile([P, T], F32, name=f"v_pool{b}") for b in range(2)]
-        for b in range(2):
-            nc.sync.dma_start(v_pool[b][:], vT[b * P:(b + 1) * P, :])
+        v_pool = [sb.tile([P, T], F32, name="v_pool0"), reuse.tile([P, T], F32, name="v_pool1", offset=0, align_bytes=64)]
+        nc.sync.dma_start(v_pool[0][:], vT[0:P, :])
+        for first, end in zip([0] + [reach(s) for s in LAST_CUTS[1:-1]], [reach(s) for s in LAST_CUTS[1:]]):
+            nc.sync.dma_start(v_pool[1][:, first:end], vT[P:2 * P, first:end])
 
         warm_in = sb.tile([P, 8], F32, name="warm_in")
         warm = sb.tile([P, 8], F32, name="warm")
         nc.vector.memset(warm_in[:], 0.0)
-        nc.scalar.activation(warm[:], warm_in[:], ACT.Tanh)
+        nc.scalar.activation(warm[:], warm_in[:], ACT.Sigmoid)
 
-        q_grp = sb.tile([P, NQ, PACK], BF16, name="q_grp", tag="k_raw1", align_bytes=64)
         q_codes = sb.tile([P, NQ], U32, name="q_codes", align_bytes=64)
         q_scales = sb.tile([P, NQ], U8, name="q_scales", align_bytes=64)
 
         k_pool = [sb.tile([P, 2 * T], BF16, name="k_pool0", align_bytes=64),
                   sb.tile([P, 2 * T], BF16, name="k_pool1", tag="k_raw0", align_bytes=64)]
         lead = SCALAR_SLOTS
-        shared = sb.tile([P, lead + N * PACK], BF16, name="shared", align_bytes=64)
+        shared = sb.tile([P, lead + (N + NQ) * PACK], BF16, name="shared", tag="k_raw1", align_bytes=64)
+        q_grp = shared[:, lead + N * PACK:].rearrange("p (n j) -> p n j", j=PACK)
         k_grp = shared[:, lead:lead + N * PACK]
         v_g = [shared[:, 0:N], shared[:, N:2 * N]]
         k_g = sb.tile([P, 2, 2 * N], BF16, name="k_g", align_bytes=64)
@@ -97,9 +101,10 @@ def tile_attend_x_sigmoid_cap_srt_kernel(tc, qT, kT, vT, vs, offs, out):
         vs_g = sb.tile([P, N], F32, name="vs_g")
         nc.vector.tensor_copy(vs_g[:].bitcast(U32).rearrange("p (t m) -> p m t", t=PACK),
                               vs_pool[:].bitcast(U32).indirect(offsets[:]))
-        vs_ps = ps.tile([P, PACK, P], F32, name="vs_ps")
-        for t in range(PACK):
-            nc.tensor.transpose(vs_ps[:, t, :], vs_g[:, t * P:(t + 1) * P], ident[:])
+        vs_ps = ps.tile([P, P + PACK], F32, name="vs_ps")
+        for t in reversed(range(PACK)):
+            nc.tensor.transpose(vs_ps[:, t + 1:t + 1 + P], vs_g[:, t * P:(t + 1) * P], ident[:])
+        vs_turned = vs_ps[:, P:P + PACK]
 
         cast_keys(scalar_cast, 0, 0, 256)
         cast_keys(nc.vector.tensor_copy, 0, 256, reach(QUARTER))
@@ -108,10 +113,9 @@ def tile_attend_x_sigmoid_cap_srt_kernel(tc, qT, kT, vT, vs, offs, out):
         gather_keys(0, 0, QUARTER)
         gather_keys(0, QUARTER, HALF)
         gather_keys(0, HALF, N)
-        cast_keys(scalar_cast, 1, 0, 384)
-        cast_keys(nc.vector.tensor_copy, 1, 384, EARLY)
-        cast_keys(nc.vector.tensor_copy, 1, EARLY, reach(QUARTER))
-        cast_keys(nc.vector.tensor_copy, 1, reach(QUARTER), reach(HALF))
+        cast_keys(scalar_cast, 1, 0, 224)
+        cast_keys(nc.vector.tensor_copy, 1, 224, reach(QUARTER))
+        cast_keys(scalar_cast, 1, reach(QUARTER), reach(HALF))
         cast_keys(scalar_cast, 1, reach(HALF), reach(HALF + QUARTER))
         cast_keys(scalar_cast, 1, reach(HALF + QUARTER), T)
         for s0 in range(0, N, QUARTER):
@@ -124,78 +128,95 @@ def tile_attend_x_sigmoid_cap_srt_kernel(tc, qT, kT, vT, vs, offs, out):
             nc.vector.quantize_mx(out=q_codes[:, cols].bitcast(FP8X4), scales=q_scales[:, cols],
                                   in_=q_grp[:, cols, :].rearrange("p n j -> p (n j)"))
 
-        for s0 in range(0, N - QUARTER, QUARTER):
-            join_keys(s0, s0 + QUARTER, 0, PACK)
-        for t0 in (2, 0):
-            join_keys(N - QUARTER, N, t0, t0 + 2)
+        join_keys(0, HALF, 2, PACK)
+        join_keys(HALF, N - QUARTER, 2, PACK)
+        join_keys(0, QUARTER, 0, 2)
+        join_keys(N - QUARTER, N, 2, PACK)
+        join_keys(QUARTER, N, 0, 2)
 
-        score_ps = [ps.tile([P, 2, NQ], F32, name=f"score_ps{i}") for i in range(2)]
+        score_ps = [ps.tile([P, NQ], F32, name=f"score_ps{t}", tag=f"bank{t}") for t in range(PACK)]
         for t in reversed(range(PACK)):
             cols = slice(t * P, (t + 1) * P)
             nc.vector.quantize_mx(out=k_codes[:, cols].bitcast(FP8X4), scales=k_scales[:, cols],
                                   in_=k_grp[:, t * P * PACK:(t + 1) * P * PACK])
         for t in reversed(range(PACK)):
             cols = slice(t * P, (t + 1) * P)
-            nc.tensor.matmul_mx(out=score_ps[t // 2][:, t % 2, :], lhsT=k_codes[:, cols].bitcast(FP8X4),
+            nc.tensor.matmul_mx(out=score_ps[t][:], lhsT=k_codes[:, cols].bitcast(FP8X4),
                                 lhsT_scale=k_scales[:, cols], rhs=q_codes[:].bitcast(FP8X4),
                                 rhs_scale=q_scales[:], start=True, stop=True)
 
         v_ps = [ps.tile([P, 2, P], F32, name=f"v_ps{b}") for b in range(2)]
         v_scales = [sb.tile([P, P], U8, name=f"v_scales{b}", align_bytes=64) for b in range(2)]
-        v_codes = [sb.tile([P, P], U32, name=f"v_codes{b}", align_bytes=64) for b in range(2)]
-        v_grp = [sb.tile([P, P * PACK], BF16, name=f"v_grp{b}", align_bytes=64) for b in range(2)]
+        v_codes = [reuse.tile([P, P], U32, name="v_codes0", offset=2 * NQ * PACK, align_bytes=64),
+                   reuse.tile([P, P], U32, name="v_codes1", offset=0, align_bytes=64)]
+        capped = [sb.tile([P, 2, NQ], F32, name=f"capped{i}", tag=f"capped{i}", align_bytes=64) for i in range(2)]
+        v_grp = [sb.tile([P, P * PACK], BF16, name="v_grp0", tag="capped1", align_bytes=64),
+                 sb.tile([P, P * PACK], BF16, name="v_grp1", align_bytes=64)]
 
-        def turn_values(b):
-            words = v_g[b].bitcast(F32)
+        def turn_values(b, planes):
             for w in range(2):
-                nc.tensor.transpose(v_ps[b][:, w, :], words[:, w:2 * P:2], ident[:])
+                nc.tensor.transpose(v_ps[b][:, w, :], planes[w], ident[:])
 
         scalar_cast(v_g[0][:, 0:SCALAR_SLOTS], v_pool[0][:].indirect(offsets[:, 0:SCALAR_SLOTS // GROUP]))
         nc.vector.tensor_copy(v_g[0][:, SCALAR_SLOTS:N],
                               v_pool[0][:].indirect(offsets[:, SCALAR_SLOTS // GROUP:N // GROUP]))
-        turn_values(0)
-        nc.vector.tensor_copy(v_g[1], v_pool[1][:].indirect(offsets[:]))
-        turn_values(1)
+        words = [v_g[b].bitcast(F32) for b in range(2)]
+        turn_values(0, [words[0][:, w:2 * P:2] for w in range(2)])
+        dealt = v_g[1].rearrange("p (w m s) -> p m w s", w=2, s=2)
+        for s0, s1 in zip(LAST_CUTS, LAST_CUTS[1:]):
+            nc.vector.tensor_copy(dealt[:, s0 // PACK:s1 // PACK, :, :],
+                                  v_pool[1][:, 0:reach(s1)].indirect(offsets[:, s0 // GROUP:s1 // GROUP]))
+        turn_values(1, [words[1][:, w * P:(w + 1) * P] for w in range(2)])
 
-        quarter_q = NQ // 4
-        capped = sb.tile([P, 2, NQ, 2], F32, name="capped")
-        centred = [sb.tile([P, quarter_q, PACK], F32, name=f"centred{c}") for c in range(4)]
-        w_grp = sb.tile([P, NQ, PACK], BF16, name="w_grp", align_bytes=64)
+        quarters = [slice(c * NQ // 4, (c + 1) * NQ // 4) for c in range(4)]
+        prob = sb.tile([P, 2, NQ, 2], F32, name="prob")
+        w_grp = [reuse.tile([P, NQ // 2, PACK], BF16, name=f"w_grp{h}", offset=h * NQ * PACK, align_bytes=64)
+                 for h in range(2)]
         w_codes = sb.tile([P, NQ], U32, name="w_codes", align_bytes=64)
         w_scales = sb.tile([P, NQ], U8, name="w_scales", align_bytes=64)
 
-        def cap(i, cols):
-            nc.scalar.activation(capped[:, i, cols, :], score_ps[i][:, :, cols].rearrange("p s n -> p n s"),
-                                 ACT.Tanh, scale=0.5)
+        def sigmoid(i, cols):
+            nc.scalar.activation(prob[:, i, cols, :], capped[i][:, :, cols].rearrange("p s n -> p n s"),
+                                 ACT.Sigmoid, scale=2.0)
 
-        cap(1, slice(0, NQ))
-        for cols in query_halves:
-            cap(0, cols)
-        for c in range(4):
-            cols = slice(c * quarter_q, (c + 1) * quarter_q)
-            nc.scalar.activation(centred[c][:].rearrange("p n (i s) -> p n i s", i=2),
-                                 capped[:, :, cols, :].rearrange("p i n s -> p n i s"), ACT.Tanh)
-        for b in range(2):
-            nc.scalar.copy(v_grp[b][:].bitcast(F32).rearrange("p (e w) -> p e w", w=2),
-                           v_ps[b][:].rearrange("p w e -> p e w"))
-        for c in range(4):
-            cols = slice(c * quarter_q, (c + 1) * quarter_q)
-            nc.vector.scalar_tensor_tensor(w_grp[:, cols, :], centred[c][:], 1.0,
-                                           vs_ps[:, :, P - 1].unsqueeze(1).to_broadcast([P, quarter_q, PACK]),
-                                           ALU.add, ALU.mult)
-        for cols in query_halves:
+        for t in reversed(range(PACK)):
+            nc.scalar.activation(capped[t // 2][:, t % 2, :], score_ps[t][:], ACT.Tanh, scale=0.5)
+        sigmoid(1, slice(0, NQ))
+        for cols in quarters:
+            sigmoid(0, cols)
+
+        def leave_psum(b, features):
+            nc.scalar.copy(v_grp[b][:].bitcast(F32).rearrange("p (e w) -> p e w", w=2)[:, features, :],
+                           v_ps[b][:].rearrange("p w e -> p e w")[:, features, :])
+
+        def quantise_values(b, features):
+            nc.vector.quantize_mx(out=v_codes[b][:, features].bitcast(FP8X4), scales=v_scales[b][:, features],
+                                  in_=v_grp[b][:, features.start * PACK:features.stop * PACK])
+
+        pieces = [(0, slice(0, P)), (1, slice(0, P // 2)), (1, slice(P // 2, P))]
+        for b, features in pieces:
+            leave_psum(b, features)
+        scales = vs_turned.rearrange("p (i s) -> p i s", i=2).unsqueeze(1).to_broadcast([P, NQ // 4, 2, 2])
+        for c, cols in enumerate(quarters):
+            nc.vector.tensor_tensor(w_grp[c // 2][:, quarters[c % 2], :].rearrange("p n (i s) -> p n i s", i=2),
+                                    prob[:, :, cols, :].rearrange("p i n s -> p n i s"), scales, ALU.mult)
+        for h, cols in enumerate(query_halves):
             nc.vector.quantize_mx(out=w_codes[:, cols].bitcast(FP8X4), scales=w_scales[:, cols],
-                                  in_=w_grp[:, cols, :].rearrange("p n t -> p (n t)"))
-        for b in range(2):
-            nc.vector.quantize_mx(out=v_codes[b][:].bitcast(FP8X4), scales=v_scales[b][:], in_=v_grp[b][:])
+                                  in_=w_grp[h][:].rearrange("p n t -> p (n t)"))
+        for b, features in pieces:
+            quantise_values(b, features)
 
-        y_ps = [ps.tile([P, P], F32, name=f"y_ps{b}") for b in range(2)]
         y = sb.tile([P, DV], F32, name="y")
-        for b in range(2):
-            nc.tensor.matmul_mx(out=y_ps[b][:], lhsT=w_codes[:].bitcast(FP8X4), lhsT_scale=w_scales[:],
-                                rhs=v_codes[b][:].bitcast(FP8X4), rhs_scale=v_scales[b][:],
+        for k, (b, features) in enumerate(pieces):
+            width = features.stop - features.start
+            y_ps = ps.tile([P, width], F32, name=f"y_ps{k}", tag=f"bank{k}")
+            nc.tensor.matmul_mx(out=y_ps[:], lhsT=w_codes[:].bitcast(FP8X4), lhsT_scale=w_scales[:],
+                                rhs=v_codes[b][:, features].bitcast(FP8X4), rhs_scale=v_scales[b][:, features],
                                 start=True, stop=True)
-        nc.vector.tensor_scalar(y[:, 0:P], y_ps[0][:], 1.0 / 32.0, None, ALU.mult)
-        nc.scalar.activation(y[:, P:DV], y_ps[1][:], ACT.Copy, scale=1.0 / 32.0)
+            dst = y[:, b * P + features.start:b * P + features.stop]
+            if b == 0:
+                nc.vector.tensor_scalar(dst, y_ps[:], 1.0 / 16.0, None, ALU.mult)
+            else:
+                nc.scalar.activation(dst, y_ps[:], ACT.Copy, scale=1.0 / 16.0)
         nc.sync.dma_start(out[0, :, 0:P], y[:, 0:P])
         nc.scalar.dma_start(out[0, :, P:DV], y[:, P:DV])

@@ -24,7 +24,6 @@ QUARTER = N // 4
 SCALAR_TOKENS = 192
 EARLY = T // 2
 SCALAR_SLOTS = 320
-LAST_CUTS = [0, 128, 320, 512]
 
 
 def reach(slots):
@@ -56,9 +55,8 @@ def tile_attend_x_sigmoid_cap_srt_kernel(tc, qT, kT, vT, vs, offs, out):
             nc.sync.dma_start(k_raw[u][:].rearrange("p (e n) -> p e n", e=2)[:, :, first:end], k_rows[:, u, :, first:end])
         nc.sync.dma_start(q_raw[:], qT[0].rearrange("(p j) n -> p j n", j=PACK))
         v_pool = [sb.tile([P, T], F32, name="v_pool0"), reuse.tile([P, T], F32, name="v_pool1", offset=0, align_bytes=64)]
-        nc.sync.dma_start(v_pool[0][:], vT[0:P, :])
-        for first, end in zip([0] + [reach(s) for s in LAST_CUTS[1:-1]], [reach(s) for s in LAST_CUTS[1:]]):
-            nc.sync.dma_start(v_pool[1][:, first:end], vT[P:2 * P, first:end])
+        for b in range(2):
+            nc.sync.dma_start(v_pool[b][:], vT[b * P:(b + 1) * P, :])
 
         warm_in = sb.tile([P, 8], F32, name="warm_in")
         warm = sb.tile([P, 8], F32, name="warm")
@@ -162,10 +160,7 @@ def tile_attend_x_sigmoid_cap_srt_kernel(tc, qT, kT, vT, vs, offs, out):
                               v_pool[0][:].indirect(offsets[:, SCALAR_SLOTS // GROUP:N // GROUP]))
         words = [v_g[b].bitcast(F32) for b in range(2)]
         turn_values(0, [words[0][:, w:2 * P:2] for w in range(2)])
-        dealt = v_g[1].rearrange("p (w m s) -> p m w s", w=2, s=2)
-        for s0, s1 in zip(LAST_CUTS, LAST_CUTS[1:]):
-            nc.vector.tensor_copy(dealt[:, s0 // PACK:s1 // PACK, :, :],
-                                  v_pool[1][:, 0:reach(s1)].indirect(offsets[:, s0 // GROUP:s1 // GROUP]))
+        nc.vector.tensor_copy(v_g[1].rearrange("p (w m s) -> p m w s", w=2, s=2), v_pool[1][:].indirect(offsets[:]))
         turn_values(1, [words[1][:, w * P:(w + 1) * P] for w in range(2)])
 
         quarters = [slice(c * NQ // 4, (c + 1) * NQ // 4) for c in range(4)]

@@ -10,6 +10,7 @@ BYTES = 4 * (D * NQ + D * T + DV * T + T + NQ * DV) + 2 * 128 * (N // 16)
 F32 = mybir.dt.float32
 BF16 = mybir.dt.bfloat16
 U32 = mybir.dt.uint32
+I32 = mybir.dt.int32
 U16 = mybir.dt.uint16
 U8 = mybir.dt.uint8
 FP8X4 = mybir.dt.float8_e4m3fn_x4
@@ -23,7 +24,7 @@ HALF = N // 2
 QUARTER = N // 4
 SCALAR_TOKENS = 192
 EARLY = T // 2
-SCALAR_SLOTS = 320
+SCALAR_SLOTS = 512
 
 
 def reach(slots):
@@ -44,14 +45,12 @@ def tile_attend_x_sigmoid_cap_srt_kernel(tc, qT, kT, vT, vs, offs, out):
         ident = sb.tile([P, P], F32, name="ident")
         make_identity(nc, ident[:])
 
-        q_raw = sb.tile([P, PACK, NQ], F32, name="q_raw")
+        q_raw = sb.tile([P, PACK, NQ], F32, name="q_raw", tag="q_raw", align_bytes=64)
         k_rows = kT.rearrange("(p u e) n -> p u e n", u=2, e=2)
         k_raw = [sb.tile([P, 2 * T], F32, name=f"k_raw{u}", tag=f"k_raw{u}", align_bytes=64) for u in range(2)]
         nc.scalar.dma_start(vs_pool[P - 1:P, :], vs[0:1, :])
         nc.sync.dma_start(offsets[:], offs)
-        for u, first, end in [(0, 0, reach(HALF)), (0, reach(HALF), T),
-                              (1, 0, reach(QUARTER)), (1, reach(QUARTER), reach(N - QUARTER)),
-                              (1, reach(N - QUARTER), T)]:
+        for u, first, end in [(0, 0, T), (1, 0, reach(HALF)), (1, reach(HALF), T)]:
             nc.sync.dma_start(k_raw[u][:].rearrange("p (e n) -> p e n", e=2)[:, :, first:end], k_rows[:, u, :, first:end])
         nc.sync.dma_start(q_raw[:], qT[0].rearrange("(p j) n -> p j n", j=PACK))
         v_pool = [sb.tile([P, T], F32, name="v_pool0"), reuse.tile([P, T], F32, name="v_pool1", offset=0, align_bytes=64)]
@@ -68,17 +67,20 @@ def tile_attend_x_sigmoid_cap_srt_kernel(tc, qT, kT, vT, vs, offs, out):
 
         k_pool = [sb.tile([P, 2 * T], BF16, name="k_pool0", align_bytes=64),
                   sb.tile([P, 2 * T], BF16, name="k_pool1", tag="k_raw0", align_bytes=64)]
-        lead = SCALAR_SLOTS
-        shared = sb.tile([P, lead + (N + NQ) * PACK], BF16, name="shared", tag="k_raw1", align_bytes=64)
-        q_grp = shared[:, lead + N * PACK:].rearrange("p (n j) -> p n j", j=PACK)
-        k_grp = shared[:, lead:lead + N * PACK]
-        v_g = [shared[:, 0:N], shared[:, N:2 * N]]
+        q_grp = sb.tile([P, NQ, PACK], BF16, name="q_grp", align_bytes=64)
+        k_tile = sb.tile([P, N * PACK], BF16, name="k_tile", tag="q_raw", align_bytes=64)
+        k_grp = k_tile[:]
+        v_tiles = [sb.tile([P, N], BF16, name=f"v_g{b}", align_bytes=64) for b in range(2)]
+        v_g = [v_tiles[b][:] for b in range(2)]
         k_g = sb.tile([P, 2, 2 * N], BF16, name="k_g", align_bytes=64)
         k_codes = sb.tile([P, N], U32, name="k_codes", align_bytes=64)
         k_scales = sb.tile([P, N], U8, name="k_scales", align_bytes=64)
 
         def scalar_cast(dst, src):
             nc.scalar.activation(dst, src, ACT.Copy)
+
+        def vector_copy(dst, src):
+            nc.vector.tensor_copy(dst, src)
 
         def cast_keys(cast, u, n0, n1):
             cast(k_pool[u][:].rearrange("p (n e) -> p n e", e=2)[:, n0:n1, :],
@@ -90,11 +92,11 @@ def tile_attend_x_sigmoid_cap_srt_kernel(tc, qT, kT, vT, vs, offs, out):
             nc.vector.tensor_copy(dst[:, s0 // PACK:s1 // PACK, :],
                                   window.indirect(offsets[:, s0 // GROUP:s1 // GROUP]))
 
-        def join_keys(s0, s1, t0, t1):
-            src = k_g[:].bitcast(U32).rearrange("p u (t m) -> p t m u", t=PACK)
-            dst = k_grp.bitcast(U32).rearrange("p (t m u) -> p t m u", t=PACK, u=2)
+        def join_keys(copy, s0, s1, t0, t1):
+            src = k_g[:].bitcast(I32 if copy is vector_copy else U32).rearrange("p u (t m) -> p t m u", t=PACK)
+            dst = k_grp.bitcast(I32 if copy is vector_copy else U32).rearrange("p (t m u) -> p t m u", t=PACK, u=2)
             columns = slice(s0 // PACK, s1 // PACK)
-            nc.scalar.copy(dst[:, t0:t1, columns, :], src[:, t0:t1, columns, :])
+            copy(dst[:, t0:t1, columns, :], src[:, t0:t1, columns, :])
 
         vs_g = sb.tile([P, N], F32, name="vs_g")
         nc.vector.tensor_copy(vs_g[:].bitcast(U32).rearrange("p (t m) -> p m t", t=PACK),
@@ -104,33 +106,23 @@ def tile_attend_x_sigmoid_cap_srt_kernel(tc, qT, kT, vT, vs, offs, out):
             nc.tensor.transpose(vs_ps[:, t + 1:t + 1 + P], vs_g[:, t * P:(t + 1) * P], ident[:])
         vs_turned = vs_ps[:, P:P + PACK]
 
-        cast_keys(scalar_cast, 0, 0, 256)
-        cast_keys(nc.vector.tensor_copy, 0, 256, reach(QUARTER))
-        cast_keys(nc.vector.tensor_copy, 0, reach(QUARTER), reach(HALF))
-        cast_keys(scalar_cast, 0, reach(HALF), T)
-        gather_keys(0, 0, QUARTER)
-        gather_keys(0, QUARTER, HALF)
-        gather_keys(0, HALF, N)
-        cast_keys(scalar_cast, 1, 0, 224)
-        cast_keys(nc.vector.tensor_copy, 1, 224, reach(QUARTER))
-        cast_keys(scalar_cast, 1, reach(QUARTER), reach(HALF))
-        cast_keys(scalar_cast, 1, reach(HALF), reach(HALF + QUARTER))
-        cast_keys(scalar_cast, 1, reach(HALF + QUARTER), T)
-        for s0 in range(0, N, QUARTER):
-            gather_keys(1, s0, s0 + QUARTER)
+        cast_keys(scalar_cast, 0, 0, 384)
+        cast_keys(vector_copy, 0, 384, T)
+        gather_keys(0, 0, N)
+        cast_keys(scalar_cast, 1, 0, 384)
+        cast_keys(vector_copy, 1, 384, reach(HALF))
+        cast_keys(scalar_cast, 1, reach(HALF), T)
+        for s0 in range(0, N, HALF):
+            gather_keys(1, s0, s0 + HALF)
 
         query_halves = [slice(0, NQ // 2), slice(NQ // 2, NQ)]
-        for cols in query_halves:
-            nc.vector.tensor_copy(q_grp[:, cols, :], q_raw[:, :, cols].rearrange("p j n -> p n j"))
-        for cols in query_halves:
-            nc.vector.quantize_mx(out=q_codes[:, cols].bitcast(FP8X4), scales=q_scales[:, cols],
-                                  in_=q_grp[:, cols, :].rearrange("p n j -> p (n j)"))
-
-        join_keys(0, HALF, 2, PACK)
-        join_keys(HALF, N - QUARTER, 2, PACK)
-        join_keys(0, QUARTER, 0, 2)
-        join_keys(N - QUARTER, N, 2, PACK)
-        join_keys(QUARTER, N, 0, 2)
+        scalar_cast(q_grp[:], q_raw[:].rearrange("p j n -> p n j"))
+        join_keys(vector_copy, 0, HALF, 2, PACK)
+        nc.vector.quantize_mx(out=q_codes[:].bitcast(FP8X4), scales=q_scales[:],
+                              in_=q_grp[:].rearrange("p n j -> p (n j)"))
+        join_keys(vector_copy, HALF, N, 2, PACK)
+        for s0 in range(0, N, HALF):
+            join_keys(nc.scalar.copy, s0, s0 + HALF, 0, 2)
 
         score_ps = [ps.tile([P, NQ], F32, name=f"score_ps{t}", tag=f"bank{t}") for t in range(PACK)]
         for t in reversed(range(PACK)):
@@ -143,7 +135,7 @@ def tile_attend_x_sigmoid_cap_srt_kernel(tc, qT, kT, vT, vs, offs, out):
                                 lhsT_scale=k_scales[:, cols], rhs=q_codes[:].bitcast(FP8X4),
                                 rhs_scale=q_scales[:], start=True, stop=True)
 
-        v_ps = [ps.tile([P, 2, P], F32, name=f"v_ps{b}") for b in range(2)]
+        v_ps = [ps.tile([P, 2, P], F32, name="v_ps0", tag="bank3"), ps.tile([P, 2, P], F32, name="v_ps1")]
         v_scales = [sb.tile([P, P], U8, name=f"v_scales{b}", align_bytes=64) for b in range(2)]
         v_codes = [reuse.tile([P, P], U32, name="v_codes0", offset=2 * NQ * PACK, align_bytes=64),
                    reuse.tile([P, P], U32, name="v_codes1", offset=0, align_bytes=64)]
@@ -155,9 +147,7 @@ def tile_attend_x_sigmoid_cap_srt_kernel(tc, qT, kT, vT, vs, offs, out):
             for w in range(2):
                 nc.tensor.transpose(v_ps[b][:, w, :], planes[w], ident[:])
 
-        scalar_cast(v_g[0][:, 0:SCALAR_SLOTS], v_pool[0][:].indirect(offsets[:, 0:SCALAR_SLOTS // GROUP]))
-        nc.vector.tensor_copy(v_g[0][:, SCALAR_SLOTS:N],
-                              v_pool[0][:].indirect(offsets[:, SCALAR_SLOTS // GROUP:N // GROUP]))
+        scalar_cast(v_g[0], v_pool[0][:].indirect(offsets[:]))
         words = [v_g[b].bitcast(F32) for b in range(2)]
         turn_values(0, [words[0][:, w:2 * P:2] for w in range(2)])
         nc.vector.tensor_copy(v_g[1].rearrange("p (w m s) -> p m w s", w=2, s=2), v_pool[1][:].indirect(offsets[:]))

@@ -24,7 +24,7 @@ HALF = N // 2
 QUARTER = N // 4
 SCALAR_TOKENS = 192
 EARLY = T // 2
-SCALAR_SLOTS = 512
+SCALAR_SLOTS = 288
 
 
 def reach(slots):
@@ -50,7 +50,8 @@ def tile_attend_x_sigmoid_cap_srt_kernel(tc, qT, kT, vT, vs, offs, out):
         k_raw = [sb.tile([P, 2 * T], F32, name=f"k_raw{u}", tag=f"k_raw{u}", align_bytes=64) for u in range(2)]
         nc.scalar.dma_start(vs_pool[P - 1:P, :], vs[0:1, :])
         nc.sync.dma_start(offsets[:], offs)
-        for u, first, end in [(0, 0, T), (1, 0, reach(HALF)), (1, reach(HALF), T)]:
+        for u, first, end in [(0, 0, reach(HALF)), (0, reach(HALF), T),
+                              (1, 0, EARLY), (1, EARLY, reach(N - QUARTER)), (1, reach(N - QUARTER), T)]:
             nc.sync.dma_start(k_raw[u][:].rearrange("p (e n) -> p e n", e=2)[:, :, first:end], k_rows[:, u, :, first:end])
         nc.sync.dma_start(q_raw[:], qT[0].rearrange("(p j) n -> p j n", j=PACK))
         v_pool = [sb.tile([P, T], F32, name="v_pool0"), reuse.tile([P, T], F32, name="v_pool1", offset=0, align_bytes=64)]
@@ -68,10 +69,10 @@ def tile_attend_x_sigmoid_cap_srt_kernel(tc, qT, kT, vT, vs, offs, out):
         k_pool = [sb.tile([P, 2 * T], BF16, name="k_pool0", align_bytes=64),
                   sb.tile([P, 2 * T], BF16, name="k_pool1", tag="k_raw0", align_bytes=64)]
         q_grp = sb.tile([P, NQ, PACK], BF16, name="q_grp", align_bytes=64)
-        k_tile = sb.tile([P, N * PACK], BF16, name="k_tile", tag="q_raw", align_bytes=64)
-        k_grp = k_tile[:]
-        v_tiles = [sb.tile([P, N], BF16, name=f"v_g{b}", align_bytes=64) for b in range(2)]
-        v_g = [v_tiles[b][:] for b in range(2)]
+        shared = sb.tile([P, SCALAR_SLOTS + N * PACK], BF16, name="shared", tag="q_raw", align_bytes=64)
+        k_grp = shared[:, SCALAR_SLOTS:]
+        v_last = sb.tile([P, N], BF16, name="v_last", align_bytes=64)
+        v_g = [shared[:, 0:N], v_last[:]]
         k_g = sb.tile([P, 2, 2 * N], BF16, name="k_g", align_bytes=64)
         k_codes = sb.tile([P, N], U32, name="k_codes", align_bytes=64)
         k_scales = sb.tile([P, N], U8, name="k_scales", align_bytes=64)
@@ -106,48 +107,56 @@ def tile_attend_x_sigmoid_cap_srt_kernel(tc, qT, kT, vT, vs, offs, out):
             nc.tensor.transpose(vs_ps[:, t + 1:t + 1 + P], vs_g[:, t * P:(t + 1) * P], ident[:])
         vs_turned = vs_ps[:, P:P + PACK]
 
-        cast_keys(scalar_cast, 0, 0, 384)
-        cast_keys(vector_copy, 0, 384, T)
-        gather_keys(0, 0, N)
+        cast_keys(scalar_cast, 0, 0, 256)
+        cast_keys(vector_copy, 0, 256, reach(HALF))
+        cast_keys(scalar_cast, 0, reach(HALF), T)
+        for s0 in range(0, N, HALF):
+            gather_keys(0, s0, s0 + HALF)
         cast_keys(scalar_cast, 1, 0, 384)
-        cast_keys(vector_copy, 1, 384, reach(HALF))
-        cast_keys(scalar_cast, 1, reach(HALF), T)
+        cast_keys(vector_copy, 1, 384, EARLY)
+        cast_keys(vector_copy, 1, EARLY, 688)
+        cast_keys(scalar_cast, 1, 688, reach(HALF))
+        cast_keys(scalar_cast, 1, reach(HALF), reach(N - QUARTER))
+        cast_keys(scalar_cast, 1, reach(N - QUARTER), T)
         for s0 in range(0, N, HALF):
             gather_keys(1, s0, s0 + HALF)
 
         query_halves = [slice(0, NQ // 2), slice(NQ // 2, NQ)]
         scalar_cast(q_grp[:], q_raw[:].rearrange("p j n -> p n j"))
-        join_keys(vector_copy, 0, HALF, 2, PACK)
+        join_keys(vector_copy, 0, HALF, 0, 2)
         nc.vector.quantize_mx(out=q_codes[:].bitcast(FP8X4), scales=q_scales[:],
                               in_=q_grp[:].rearrange("p n j -> p (n j)"))
-        join_keys(vector_copy, HALF, N, 2, PACK)
+        join_keys(vector_copy, HALF, N, 0, 2)
         for s0 in range(0, N, HALF):
-            join_keys(nc.scalar.copy, s0, s0 + HALF, 0, 2)
+            join_keys(nc.scalar.copy, s0, s0 + HALF, 2, PACK)
 
         score_ps = [ps.tile([P, NQ], F32, name=f"score_ps{t}", tag=f"bank{t}") for t in range(PACK)]
-        for t in reversed(range(PACK)):
+        tile_order = [1, 0, 3, 2]
+        for t in tile_order:
             cols = slice(t * P, (t + 1) * P)
             nc.vector.quantize_mx(out=k_codes[:, cols].bitcast(FP8X4), scales=k_scales[:, cols],
                                   in_=k_grp[:, t * P * PACK:(t + 1) * P * PACK])
-        for t in reversed(range(PACK)):
+        for t in tile_order:
             cols = slice(t * P, (t + 1) * P)
             nc.tensor.matmul_mx(out=score_ps[t][:], lhsT=k_codes[:, cols].bitcast(FP8X4),
                                 lhsT_scale=k_scales[:, cols], rhs=q_codes[:].bitcast(FP8X4),
                                 rhs_scale=q_scales[:], start=True, stop=True)
 
-        v_ps = [ps.tile([P, 2, P], F32, name="v_ps0", tag="bank3"), ps.tile([P, 2, P], F32, name="v_ps1")]
+        v_ps = [ps.tile([P, 2, P], F32, name="v_ps0", tag="bank1"), ps.tile([P, 2, P], F32, name="v_ps1")]
         v_scales = [sb.tile([P, P], U8, name=f"v_scales{b}", align_bytes=64) for b in range(2)]
-        v_codes = [reuse.tile([P, P], U32, name="v_codes0", offset=2 * NQ * PACK, align_bytes=64),
-                   reuse.tile([P, P], U32, name="v_codes1", offset=0, align_bytes=64)]
+        v_codes = [reuse.tile([P, P], U32, name="v_codes0", offset=0, align_bytes=64),
+                   reuse.tile([P, P], U32, name="v_codes1", offset=4 * T, align_bytes=64)]
         capped = [sb.tile([P, 2, NQ], F32, name=f"capped{i}", tag=f"capped{i}", align_bytes=64) for i in range(2)]
-        v_grp = [sb.tile([P, P * PACK], BF16, name="v_grp0", tag="capped1", align_bytes=64),
+        v_grp = [sb.tile([P, P * PACK], BF16, name="v_grp0", tag="capped0", align_bytes=64),
                  sb.tile([P, P * PACK], BF16, name="v_grp1", align_bytes=64)]
 
         def turn_values(b, planes):
             for w in range(2):
                 nc.tensor.transpose(v_ps[b][:, w, :], planes[w], ident[:])
 
-        scalar_cast(v_g[0], v_pool[0][:].indirect(offsets[:]))
+        scalar_cast(v_g[0][:, 0:SCALAR_SLOTS], v_pool[0][:].indirect(offsets[:, 0:SCALAR_SLOTS // GROUP]))
+        nc.vector.tensor_copy(v_g[0][:, SCALAR_SLOTS:N],
+                              v_pool[0][:].indirect(offsets[:, SCALAR_SLOTS // GROUP:N // GROUP]))
         words = [v_g[b].bitcast(F32) for b in range(2)]
         turn_values(0, [words[0][:, w:2 * P:2] for w in range(2)])
         nc.vector.tensor_copy(v_g[1].rearrange("p (w m s) -> p m w s", w=2, s=2), v_pool[1][:].indirect(offsets[:]))
@@ -155,7 +164,7 @@ def tile_attend_x_sigmoid_cap_srt_kernel(tc, qT, kT, vT, vs, offs, out):
 
         quarters = [slice(c * NQ // 4, (c + 1) * NQ // 4) for c in range(4)]
         prob = sb.tile([P, 2, NQ, 2], F32, name="prob")
-        w_grp = [reuse.tile([P, NQ // 2, PACK], BF16, name=f"w_grp{h}", offset=h * NQ * PACK, align_bytes=64)
+        w_grp = [reuse.tile([P, NQ // 2, PACK], BF16, name=f"w_grp{h}", offset=4 * T + h * NQ * PACK, align_bytes=64)
                  for h in range(2)]
         w_codes = sb.tile([P, NQ], U32, name="w_codes", align_bytes=64)
         w_scales = sb.tile([P, NQ], U8, name="w_scales", align_bytes=64)
@@ -164,11 +173,11 @@ def tile_attend_x_sigmoid_cap_srt_kernel(tc, qT, kT, vT, vs, offs, out):
             nc.scalar.activation(prob[:, i, cols, :], capped[i][:, :, cols].rearrange("p s n -> p n s"),
                                  ACT.Sigmoid, scale=2.0)
 
-        for t in reversed(range(PACK)):
+        for t in tile_order:
             nc.scalar.activation(capped[t // 2][:, t % 2, :], score_ps[t][:], ACT.Tanh, scale=0.5)
-        sigmoid(1, slice(0, NQ))
+        sigmoid(0, slice(0, NQ))
         for cols in quarters:
-            sigmoid(0, cols)
+            sigmoid(1, cols)
 
         def leave_psum(b, features):
             nc.scalar.copy(v_grp[b][:].bitcast(F32).rearrange("p (e w) -> p e w", w=2)[:, features, :],
@@ -194,7 +203,7 @@ def tile_attend_x_sigmoid_cap_srt_kernel(tc, qT, kT, vT, vs, offs, out):
         y = sb.tile([P, DV], F32, name="y")
         for k, (b, features) in enumerate(pieces):
             width = features.stop - features.start
-            y_ps = ps.tile([P, width], F32, name=f"y_ps{k}", tag=f"bank{k}")
+            y_ps = ps.tile([P, width], F32, name=f"y_ps{k}", tag=f"bank{tile_order[k + 1]}")
             nc.tensor.matmul_mx(out=y_ps[:], lhsT=w_codes[:].bitcast(FP8X4), lhsT_scale=w_scales[:],
                                 rhs=v_codes[b][:, features].bitcast(FP8X4), rhs_scale=v_scales[b][:, features],
                                 start=True, stop=True)

@@ -10,7 +10,6 @@ BYTES = 4 * (D * NQ + D * T + DV * T + T + NQ * DV) + 2 * 128 * (N // 16)
 F32 = mybir.dt.float32
 BF16 = mybir.dt.bfloat16
 U32 = mybir.dt.uint32
-I32 = mybir.dt.int32
 U16 = mybir.dt.uint16
 U8 = mybir.dt.uint8
 FP8X4 = mybir.dt.float8_e4m3fn_x4
@@ -45,7 +44,7 @@ def tile_attend_x_sigmoid_cap_srt_kernel(tc, qT, kT, vT, vs, offs, out):
         ident = sb.tile([P, P], F32, name="ident")
         make_identity(nc, ident[:])
 
-        q_raw = sb.tile([P, PACK, NQ], F32, name="q_raw", tag="q_raw", align_bytes=64)
+        q_raw = sb.tile([P, PACK, NQ], F32, name="q_raw")
         k_rows = kT.rearrange("(p u e) n -> p u e n", u=2, e=2)
         k_raw = [sb.tile([P, 2 * T], F32, name=f"k_raw{u}", tag=f"k_raw{u}", align_bytes=64) for u in range(2)]
         nc.scalar.dma_start(vs_pool[P - 1:P, :], vs[0:1, :])
@@ -69,7 +68,7 @@ def tile_attend_x_sigmoid_cap_srt_kernel(tc, qT, kT, vT, vs, offs, out):
         k_pool = [sb.tile([P, 2 * T], BF16, name="k_pool0", align_bytes=64),
                   sb.tile([P, 2 * T], BF16, name="k_pool1", tag="k_raw0", align_bytes=64)]
         q_grp = sb.tile([P, NQ, PACK], BF16, name="q_grp", align_bytes=64)
-        shared = sb.tile([P, SCALAR_SLOTS + N * PACK], BF16, name="shared", tag="q_raw", align_bytes=64)
+        shared = sb.tile([P, SCALAR_SLOTS + N * PACK], BF16, name="shared", align_bytes=64)
         k_grp = shared[:, SCALAR_SLOTS:]
         v_last = sb.tile([P, N], BF16, name="v_last", align_bytes=64)
         v_g = [shared[:, 0:N], v_last[:]]
@@ -93,11 +92,11 @@ def tile_attend_x_sigmoid_cap_srt_kernel(tc, qT, kT, vT, vs, offs, out):
             nc.vector.tensor_copy(dst[:, s0 // PACK:s1 // PACK, :],
                                   window.indirect(offsets[:, s0 // GROUP:s1 // GROUP]))
 
-        def join_keys(copy, s0, s1, t0, t1):
-            src = k_g[:].bitcast(I32 if copy is vector_copy else U32).rearrange("p u (t m) -> p t m u", t=PACK)
-            dst = k_grp.bitcast(I32 if copy is vector_copy else U32).rearrange("p (t m u) -> p t m u", t=PACK, u=2)
+        def join_keys(s0, s1, t0, t1):
+            src = k_g[:].bitcast(U32).rearrange("p u (t m) -> p t m u", t=PACK)
+            dst = k_grp.bitcast(U32).rearrange("p (t m u) -> p t m u", t=PACK, u=2)
             columns = slice(s0 // PACK, s1 // PACK)
-            copy(dst[:, t0:t1, columns, :], src[:, t0:t1, columns, :])
+            nc.scalar.copy(dst[:, t0:t1, columns, :], src[:, t0:t1, columns, :])
 
         vs_g = sb.tile([P, N], F32, name="vs_g")
         nc.vector.tensor_copy(vs_g[:].bitcast(U32).rearrange("p (t m) -> p m t", t=PACK),
@@ -122,16 +121,17 @@ def tile_attend_x_sigmoid_cap_srt_kernel(tc, qT, kT, vT, vs, offs, out):
             gather_keys(1, s0, s0 + HALF)
 
         query_halves = [slice(0, NQ // 2), slice(NQ // 2, NQ)]
-        scalar_cast(q_grp[:], q_raw[:].rearrange("p j n -> p n j"))
-        join_keys(vector_copy, 0, HALF, 0, 2)
-        nc.vector.quantize_mx(out=q_codes[:].bitcast(FP8X4), scales=q_scales[:],
-                              in_=q_grp[:].rearrange("p n j -> p (n j)"))
-        join_keys(vector_copy, HALF, N, 0, 2)
-        for s0 in range(0, N, HALF):
-            join_keys(nc.scalar.copy, s0, s0 + HALF, 2, PACK)
+        for cols in query_halves:
+            nc.vector.tensor_copy(q_grp[:, cols, :], q_raw[:, :, cols].rearrange("p j n -> p n j"))
+        for cols in query_halves:
+            nc.vector.quantize_mx(out=q_codes[:, cols].bitcast(FP8X4), scales=q_scales[:, cols],
+                                  in_=q_grp[:, cols, :].rearrange("p n j -> p (n j)"))
+        tile_order = [1, 0, 3, 2]
+        join_keys(0, HALF, 0, PACK)
+        for t in tile_order:
+            join_keys(HALF, N, t, t + 1)
 
         score_ps = [ps.tile([P, NQ], F32, name=f"score_ps{t}", tag=f"bank{t}") for t in range(PACK)]
-        tile_order = [1, 0, 3, 2]
         for t in tile_order:
             cols = slice(t * P, (t + 1) * P)
             nc.vector.quantize_mx(out=k_codes[:, cols].bitcast(FP8X4), scales=k_scales[:, cols],
@@ -146,7 +146,7 @@ def tile_attend_x_sigmoid_cap_srt_kernel(tc, qT, kT, vT, vs, offs, out):
         v_scales = [sb.tile([P, P], U8, name=f"v_scales{b}", align_bytes=64) for b in range(2)]
         v_codes = [reuse.tile([P, P], U32, name="v_codes0", offset=0, align_bytes=64),
                    reuse.tile([P, P], U32, name="v_codes1", offset=4 * T, align_bytes=64)]
-        capped = [sb.tile([P, 2, NQ], F32, name=f"capped{i}", tag=f"capped{i}", align_bytes=64) for i in range(2)]
+        capped = [sb.tile([P, 2, NQ + 4], F32, name=f"capped{i}", tag=f"capped{i}", align_bytes=64) for i in range(2)]
         v_grp = [sb.tile([P, P * PACK], BF16, name="v_grp0", tag="capped0", align_bytes=64),
                  sb.tile([P, P * PACK], BF16, name="v_grp1", align_bytes=64)]
 
@@ -163,7 +163,7 @@ def tile_attend_x_sigmoid_cap_srt_kernel(tc, qT, kT, vT, vs, offs, out):
         turn_values(1, [words[1][:, w * P:(w + 1) * P] for w in range(2)])
 
         quarters = [slice(c * NQ // 4, (c + 1) * NQ // 4) for c in range(4)]
-        prob = sb.tile([P, 2, NQ, 2], F32, name="prob")
+        prob = sb.tile([P, 2, NQ + 2, 2], F32, name="prob")
         w_grp = [reuse.tile([P, NQ // 2, PACK], BF16, name=f"w_grp{h}", offset=4 * T + h * NQ * PACK, align_bytes=64)
                  for h in range(2)]
         w_codes = sb.tile([P, NQ], U32, name="w_codes", align_bytes=64)
@@ -174,7 +174,7 @@ def tile_attend_x_sigmoid_cap_srt_kernel(tc, qT, kT, vT, vs, offs, out):
                                  ACT.Sigmoid, scale=2.0)
 
         for t in tile_order:
-            nc.scalar.activation(capped[t // 2][:, t % 2, :], score_ps[t][:], ACT.Tanh, scale=0.5)
+            nc.scalar.activation(capped[t // 2][:, t % 2, 0:NQ], score_ps[t][:], ACT.Tanh, scale=0.5)
         sigmoid(0, slice(0, NQ))
         for cols in quarters:
             sigmoid(1, cols)

@@ -50,7 +50,7 @@ def tile_attend_x_sigmoid_cap_srt_kernel(tc, qT, kT, vT, vs, offs, out):
         nc.scalar.dma_start(vs_pool[P - 1:P, :], vs[0:1, :])
         nc.sync.dma_start(offsets[:], offs)
         for u, first, end in [(0, 0, reach(HALF)), (0, reach(HALF), T),
-                              (1, 0, EARLY), (1, EARLY, reach(N - QUARTER)), (1, reach(N - QUARTER), T)]:
+                              (1, 0, EARLY), (1, EARLY, reach(HALF)), (1, reach(HALF), T)]:
             nc.sync.dma_start(k_raw[u][:].rearrange("p (e n) -> p e n", e=2)[:, :, first:end], k_rows[:, u, :, first:end])
         nc.sync.dma_start(q_raw[:], qT[0].rearrange("(p j) n -> p j n", j=PACK))
         v_pool = [sb.tile([P, T], F32, name="v_pool0"), reuse.tile([P, T], F32, name="v_pool1", offset=0, align_bytes=64)]
@@ -67,7 +67,7 @@ def tile_attend_x_sigmoid_cap_srt_kernel(tc, qT, kT, vT, vs, offs, out):
 
         k_pool = [sb.tile([P, 2 * T], BF16, name="k_pool0", align_bytes=64),
                   sb.tile([P, 2 * T], BF16, name="k_pool1", tag="k_raw0", align_bytes=64)]
-        q_grp = sb.tile([P, NQ, PACK], BF16, name="q_grp", align_bytes=64)
+        q_grp = sb.tile([P, NQ, PACK], BF16, name="q_grp", tag="k_raw1", align_bytes=64)
         shared = sb.tile([P, SCALAR_SLOTS + N * PACK], BF16, name="shared", align_bytes=64)
         k_grp = shared[:, SCALAR_SLOTS:]
         v_last = sb.tile([P, N], BF16, name="v_last", align_bytes=64)
@@ -78,9 +78,6 @@ def tile_attend_x_sigmoid_cap_srt_kernel(tc, qT, kT, vT, vs, offs, out):
 
         def scalar_cast(dst, src):
             nc.scalar.activation(dst, src, ACT.Copy)
-
-        def vector_copy(dst, src):
-            nc.vector.tensor_copy(dst, src)
 
         def cast_keys(cast, u, n0, n1):
             cast(k_pool[u][:].rearrange("p (n e) -> p n e", e=2)[:, n0:n1, :],
@@ -107,18 +104,20 @@ def tile_attend_x_sigmoid_cap_srt_kernel(tc, qT, kT, vT, vs, offs, out):
         vs_turned = vs_ps[:, P:P + PACK]
 
         cast_keys(scalar_cast, 0, 0, 256)
-        cast_keys(vector_copy, 0, 256, reach(HALF))
+        cast_keys(nc.vector.tensor_copy, 0, 256, reach(QUARTER))
+        cast_keys(nc.vector.tensor_copy, 0, reach(QUARTER), reach(HALF))
         cast_keys(scalar_cast, 0, reach(HALF), T)
-        for s0 in range(0, N, HALF):
-            gather_keys(0, s0, s0 + HALF)
+        gather_keys(0, 0, QUARTER)
+        gather_keys(0, QUARTER, HALF)
+        gather_keys(0, HALF, N)
         cast_keys(scalar_cast, 1, 0, 384)
-        cast_keys(vector_copy, 1, 384, EARLY)
-        cast_keys(vector_copy, 1, EARLY, 688)
-        cast_keys(scalar_cast, 1, 688, reach(HALF))
-        cast_keys(scalar_cast, 1, reach(HALF), reach(N - QUARTER))
-        cast_keys(scalar_cast, 1, reach(N - QUARTER), T)
-        for s0 in range(0, N, HALF):
-            gather_keys(1, s0, s0 + HALF)
+        cast_keys(nc.vector.tensor_copy, 1, 384, EARLY)
+        cast_keys(nc.vector.tensor_copy, 1, EARLY, reach(QUARTER))
+        cast_keys(nc.vector.tensor_copy, 1, reach(QUARTER), reach(HALF))
+        cast_keys(scalar_cast, 1, reach(HALF), reach(HALF + QUARTER))
+        cast_keys(scalar_cast, 1, reach(HALF + QUARTER), T)
+        for s0 in range(0, N, QUARTER):
+            gather_keys(1, s0, s0 + QUARTER)
 
         query_halves = [slice(0, NQ // 2), slice(NQ // 2, NQ)]
         for cols in query_halves:
@@ -127,9 +126,10 @@ def tile_attend_x_sigmoid_cap_srt_kernel(tc, qT, kT, vT, vs, offs, out):
             nc.vector.quantize_mx(out=q_codes[:, cols].bitcast(FP8X4), scales=q_scales[:, cols],
                                   in_=q_grp[:, cols, :].rearrange("p n j -> p (n j)"))
         tile_order = [1, 0, 3, 2]
-        join_keys(0, HALF, 0, PACK)
-        for t in tile_order:
-            join_keys(HALF, N, t, t + 1)
+        for s0 in range(0, N - QUARTER, QUARTER):
+            join_keys(s0, s0 + QUARTER, 0, PACK)
+        for t0 in (0, 2):
+            join_keys(N - QUARTER, N, t0, t0 + 2)
 
         score_ps = [ps.tile([P, NQ], F32, name=f"score_ps{t}", tag=f"bank{t}") for t in range(PACK)]
         for t in tile_order:

@@ -23,7 +23,6 @@ HALF = N // 2
 QUARTER = N // 4
 SCALAR_TOKENS = 192
 EARLY = T // 2
-SCALAR_SLOTS = 288
 
 
 def reach(slots):
@@ -68,10 +67,10 @@ def tile_attend_x_sigmoid_cap_srt_kernel(tc, qT, kT, vT, vs, offs, out):
         k_pool = [sb.tile([P, 2 * T], BF16, name="k_pool0", align_bytes=64),
                   sb.tile([P, 2 * T], BF16, name="k_pool1", tag="k_raw0", align_bytes=64)]
         q_grp = sb.tile([P, NQ, PACK], BF16, name="q_grp", tag="k_raw1", align_bytes=64)
-        shared = sb.tile([P, SCALAR_SLOTS + N * PACK], BF16, name="shared", align_bytes=64)
-        k_grp = shared[:, SCALAR_SLOTS:]
-        v_last = sb.tile([P, N], BF16, name="v_last", align_bytes=64)
-        v_g = [shared[:, 0:N], v_last[:]]
+        k_tile = sb.tile([P, N * PACK], BF16, name="k_tile", align_bytes=64)
+        k_grp = k_tile[:]
+        v_tiles = [sb.tile([P, N], BF16, name=f"v_g{b}", align_bytes=64) for b in range(2)]
+        v_g = [v_tiles[b][:] for b in range(2)]
         k_g = sb.tile([P, 2, 2 * N], BF16, name="k_g", align_bytes=64)
         k_codes = sb.tile([P, N], U32, name="k_codes", align_bytes=64)
         k_scales = sb.tile([P, N], U8, name="k_scales", align_bytes=64)
@@ -154,9 +153,7 @@ def tile_attend_x_sigmoid_cap_srt_kernel(tc, qT, kT, vT, vs, offs, out):
             for w in range(2):
                 nc.tensor.transpose(v_ps[b][:, w, :], planes[w], ident[:])
 
-        scalar_cast(v_g[0][:, 0:SCALAR_SLOTS], v_pool[0][:].indirect(offsets[:, 0:SCALAR_SLOTS // GROUP]))
-        nc.vector.tensor_copy(v_g[0][:, SCALAR_SLOTS:N],
-                              v_pool[0][:].indirect(offsets[:, SCALAR_SLOTS // GROUP:N // GROUP]))
+        scalar_cast(v_g[0], v_pool[0][:].indirect(offsets[:]))
         words = [v_g[b].bitcast(F32) for b in range(2)]
         turn_values(0, [words[0][:, w:2 * P:2] for w in range(2)])
         nc.vector.tensor_copy(v_g[1].rearrange("p (w m s) -> p m w s", w=2, s=2), v_pool[1][:].indirect(offsets[:]))

@@ -37,22 +37,22 @@ def tile_attend_x_sigmoid_cap_srt_kernel(tc, qT, kT, vT, vs, offs, out):
         ps = ctx.enter_context(tc.psum_pool(name="ps", bufs=1))
 
         offsets = sb.tile([P, N // GROUP], U16, name="offsets")
-        vs_pool = sb.tile([P, T], F32, name="vs_pool")
+        vs_pool = sb.tile([P, T], F32, name="vs_pool", align_bytes=256)
         nc.vector.memset(vs_pool[0:P - 1, :], 0.0)
 
         ident = sb.tile([P, P], F32, name="ident")
         make_identity(nc, ident[:])
 
-        q_raw = sb.tile([P, PACK, NQ], F32, name="q_raw")
+        q_raw = sb.tile([P, PACK, NQ], F32, name="q_raw", align_bytes=256)
         k_rows = kT.rearrange("(p u e) n -> p u e n", u=2, e=2)
-        k_raw = [sb.tile([P, 2 * T], F32, name=f"k_raw{u}", tag=f"k_raw{u}", align_bytes=64) for u in range(2)]
+        k_raw = [sb.tile([P, 2 * T], F32, name=f"k_raw{u}", tag=f"k_raw{u}", align_bytes=256) for u in range(2)]
         nc.scalar.dma_start(vs_pool[P - 1:P, :], vs[0:1, :])
         nc.sync.dma_start(offsets[:], offs)
         for u, first, end in [(0, 0, reach(HALF)), (0, reach(HALF), T),
                               (1, 0, EARLY), (1, EARLY, reach(HALF)), (1, reach(HALF), T)]:
             nc.sync.dma_start(k_raw[u][:].rearrange("p (e n) -> p e n", e=2)[:, :, first:end], k_rows[:, u, :, first:end])
         nc.sync.dma_start(q_raw[:], qT[0].rearrange("(p j) n -> p j n", j=PACK))
-        v_pool = [sb.tile([P, T], F32, name="v_pool0"), reuse.tile([P, T], F32, name="v_pool1", offset=0, align_bytes=64)]
+        v_pool = [sb.tile([P, T], F32, name="v_pool0", align_bytes=256), reuse.tile([P, T], F32, name="v_pool1", offset=0, align_bytes=256)]
         for b in range(2):
             nc.sync.dma_start(v_pool[b][:], vT[b * P:(b + 1) * P, :])
 
@@ -65,8 +65,8 @@ def tile_attend_x_sigmoid_cap_srt_kernel(tc, qT, kT, vT, vs, offs, out):
         q_scales = sb.tile([P, NQ], U8, name="q_scales", align_bytes=64)
 
         k_pool = [sb.tile([P, 2 * T], BF16, name="k_pool0", align_bytes=64),
-                  sb.tile([P, 2 * T], BF16, name="k_pool1", tag="k_raw0", align_bytes=64)]
-        q_grp = sb.tile([P, NQ, PACK], BF16, name="q_grp", tag="k_raw1", align_bytes=64)
+                  sb.tile([P, 2 * T], BF16, name="k_pool1", tag="k_raw0", align_bytes=256)]
+        q_grp = sb.tile([P, NQ, PACK], BF16, name="q_grp", tag="k_raw1", align_bytes=256)
         k_tile = sb.tile([P, N * PACK], BF16, name="k_tile", align_bytes=64)
         k_grp = k_tile[:]
         v_tiles = [sb.tile([P, N], BF16, name=f"v_g{b}", align_bytes=64) for b in range(2)]
@@ -143,8 +143,8 @@ def tile_attend_x_sigmoid_cap_srt_kernel(tc, qT, kT, vT, vs, offs, out):
 
         v_ps = [ps.tile([P, 2, P], F32, name="v_ps0", tag="bank1"), ps.tile([P, 2, P], F32, name="v_ps1")]
         v_scales = [sb.tile([P, P], U8, name=f"v_scales{b}", align_bytes=64) for b in range(2)]
-        v_codes = [reuse.tile([P, P], U32, name="v_codes0", offset=0, align_bytes=64),
-                   reuse.tile([P, P], U32, name="v_codes1", offset=4 * T, align_bytes=64)]
+        v_codes = [reuse.tile([P, P], U32, name="v_codes0", offset=0, align_bytes=256),
+                   reuse.tile([P, P], U32, name="v_codes1", offset=4 * T, align_bytes=256)]
         capped = [sb.tile([P, 2, NQ + 4], F32, name=f"capped{i}", tag=f"capped{i}", align_bytes=64) for i in range(2)]
         v_grp = [sb.tile([P, P * PACK], BF16, name="v_grp0", tag="capped0", align_bytes=64),
                  sb.tile([P, P * PACK], BF16, name="v_grp1", align_bytes=64)]
@@ -161,7 +161,7 @@ def tile_attend_x_sigmoid_cap_srt_kernel(tc, qT, kT, vT, vs, offs, out):
 
         quarters = [slice(c * NQ // 4, (c + 1) * NQ // 4) for c in range(4)]
         prob = sb.tile([P, 2, NQ + 2, 2], F32, name="prob")
-        w_grp = [reuse.tile([P, NQ // 2, PACK], BF16, name=f"w_grp{h}", offset=4 * T + h * NQ * PACK, align_bytes=64)
+        w_grp = [reuse.tile([P, NQ // 2, PACK], BF16, name=f"w_grp{h}", offset=4 * T + h * NQ * PACK, align_bytes=256)
                  for h in range(2)]
         w_codes = sb.tile([P, NQ], U32, name="w_codes", align_bytes=64)
         w_scales = sb.tile([P, NQ], U8, name="w_scales", align_bytes=64)
@@ -197,7 +197,7 @@ def tile_attend_x_sigmoid_cap_srt_kernel(tc, qT, kT, vT, vs, offs, out):
         for b, features in pieces:
             quantise_values(b, features)
 
-        y = sb.tile([P, DV], F32, name="y")
+        y = sb.tile([P, DV], F32, name="y", align_bytes=256)
         for k, (b, features) in enumerate(pieces):
             width = features.stop - features.start
             y_ps = ps.tile([P, width], F32, name=f"y_ps{k}", tag=f"bank{tile_order[k + 1]}")

from contextlib import ExitStack

import concourse.mybir as mybir
from concourse.masks import make_identity

N, T, D, DV, NQ = 512, 1024, 512, 256, 128
FLOPS = 2 * NQ * N * D + 2 * NQ * N * DV
BYTES = 4 * (D * NQ + D * T + DV * T + T + NQ * DV) + 2 * 128 * (N // 16)

F32 = mybir.dt.float32
BF16 = mybir.dt.bfloat16
U32 = mybir.dt.uint32
U16 = mybir.dt.uint16
U8 = mybir.dt.uint8
FP8X4 = mybir.dt.float8_e4m3fn_x4
ACT = mybir.ActivationFunctionType
ALU = mybir.AluOpType

P = 128
PACK = 4
GROUP = 16
HALF = N // 2
QUARTER = N // 4
SCALAR_TOKENS = 192
EARLY = T // 2


def reach(slots):
    return T - N + slots


def tile_attend_x_sigmoid_cap_srt_kernel(tc, qT, kT, vT, vs, offs, out):
    nc = tc.nc
    with ExitStack() as ctx:
        sb = ctx.enter_context(tc.tile_pool(name="sb", bufs=1))
        reuse = ctx.enter_context(tc.tile_pool(name="reuse", bufs=1))
        ps = ctx.enter_context(tc.psum_pool(name="ps", bufs=1))

        offsets = sb.tile([P, N // GROUP], U16, name="offsets")
        vs_pool = sb.tile([P, T], F32, name="vs_pool", align_bytes=256)
        nc.vector.memset(vs_pool[0:P - 1, :], 0.0)

        ident = sb.tile([P, P], F32, name="ident")
        make_identity(nc, ident[:])

        q_raw = sb.tile([P, PACK, NQ], F32, name="q_raw", align_bytes=256)
        k_rows = kT.rearrange("(p u e) n -> p u e n", u=2, e=2)
        k_raw = [sb.tile([P, 2 * T], F32, name=f"k_raw{u}", tag=f"k_raw{u}", align_bytes=256) for u in range(2)]
        nc.scalar.dma_start(vs_pool[P - 1:P, :], vs[0:1, :])
        nc.sync.dma_start(offsets[:], offs)
        for u, first, end in [(0, 0, reach(HALF)), (0, reach(HALF), T),
                              (1, 0, EARLY), (1, EARLY, reach(HALF)), (1, reach(HALF), T)]:
            nc.sync.dma_start(k_raw[u][:].rearrange("p (e n) -> p e n", e=2)[:, :, first:end], k_rows[:, u, :, first:end])
        nc.sync.dma_start(q_raw[:], qT[0].rearrange("(p j) n -> p j n", j=PACK))
        v_pool = [sb.tile([P, T], F32, name="v_pool0", align_bytes=256), reuse.tile([P, T], F32, name="v_pool1", offset=0, align_bytes=256)]
        for b in range(2):
            nc.sync.dma_start(v_pool[b][:], vT[b * P:(b + 1) * P, :])

        warm_in = sb.tile([P, 8], F32, name="warm_in")
        warm = sb.tile([P, 8], F32, name="warm")
        nc.vector.memset(warm_in[:], 0.0)
        nc.scalar.activation(warm[:], warm_in[:], ACT.Sigmoid)

        q_codes = sb.tile([P, NQ], U32, name="q_codes", align_bytes=64)
        q_scales = sb.tile([P, NQ], U8, name="q_scales", align_bytes=64)

        k_pool = [sb.tile([P, 2 * T], BF16, name="k_pool0", align_bytes=64),
                  sb.tile([P, 2 * T], BF16, name="k_pool1", tag="k_raw0", align_bytes=256)]
        q_grp = sb.tile([P, NQ, PACK], BF16, name="q_grp", tag="k_raw1", align_bytes=256)
        k_tile = sb.tile([P, N * PACK], BF16, name="k_tile", align_bytes=64)
        k_grp = k_tile[:]
        v_tiles = [sb.tile([P, N], BF16, name=f"v_g{b}", align_bytes=64) for b in range(2)]
        v_g = [v_tiles[b][:] for b in range(2)]
        k_g = sb.tile([P, 2, 2 * N], BF16, name="k_g", align_bytes=64)
        k_codes = sb.tile([P, N], U32, name="k_codes", align_bytes=64)
        k_scales = sb.tile([P, N], U8, name="k_scales", align_bytes=64)

        def scalar_cast(dst, src):
            nc.scalar.activation(dst, src, ACT.Copy)

        def cast_keys(cast, u, n0, n1):
            cast(k_pool[u][:].rearrange("p (n e) -> p n e", e=2)[:, n0:n1, :],
                 k_raw[u][:].rearrange("p (e n) -> p n e", e=2)[:, n0:n1, :])

        def gather_keys(u, s0, s1):
            window = k_pool[u][:].bitcast(U32)[:, 0:reach(s1)]
            dst = k_g[:, u, :].bitcast(U32).rearrange("p (t m) -> p m t", t=PACK)
            nc.vector.tensor_copy(dst[:, s0 // PACK:s1 // PACK, :],
                                  window.indirect(offsets[:, s0 // GROUP:s1 // GROUP]))

        def join_keys(s0, s1, t0, t1):
            src = k_g[:].bitcast(U32).rearrange("p u (t m) -> p t m u", t=PACK)
            dst = k_grp.bitcast(U32).rearrange("p (t m u) -> p t m u", t=PACK, u=2)
            columns = slice(s0 // PACK, s1 // PACK)
            nc.scalar.copy(dst[:, t0:t1, columns, :], src[:, t0:t1, columns, :])

        vs_g = sb.tile([P, N], F32, name="vs_g")
        nc.vector.tensor_copy(vs_g[:].bitcast(U32).rearrange("p (t m) -> p m t", t=PACK),
                              vs_pool[:].bitcast(U32).indirect(offsets[:]))
        vs_ps = ps.tile([P, P + PACK], F32, name="vs_ps")
        for t in reversed(range(PACK)):
            nc.tensor.transpose(vs_ps[:, t + 1:t + 1 + P], vs_g[:, t * P:(t + 1) * P], ident[:])
        vs_turned = vs_ps[:, P:P + PACK]

        cast_keys(scalar_cast, 0, 0, 256)
        cast_keys(nc.vector.tensor_copy, 0, 256, reach(QUARTER))
        cast_keys(nc.vector.tensor_copy, 0, reach(QUARTER), reach(HALF))
        cast_keys(scalar_cast, 0, reach(HALF), T)
        gather_keys(0, 0, QUARTER)
        gather_keys(0, QUARTER, HALF)
        gather_keys(0, HALF, N)
        cast_keys(scalar_cast, 1, 0, 384)
        cast_keys(nc.vector.tensor_copy, 1, 384, EARLY)
        cast_keys(nc.vector.tensor_copy, 1, EARLY, reach(QUARTER))
        cast_keys(nc.vector.tensor_copy, 1, reach(QUARTER), reach(HALF))
        cast_keys(scalar_cast, 1, reach(HALF), reach(HALF + QUARTER))
        cast_keys(scalar_cast, 1, reach(HALF + QUARTER), T)
        for s0 in range(0, N, QUARTER):
            gather_keys(1, s0, s0 + QUARTER)

        query_halves = [slice(0, NQ // 2), slice(NQ // 2, NQ)]
        for cols in query_halves:
            nc.vector.tensor_copy(q_grp[:, cols, :], q_raw[:, :, cols].rearrange("p j n -> p n j"))
        for cols in query_halves:
            nc.vector.quantize_mx(out=q_codes[:, cols].bitcast(FP8X4), scales=q_scales[:, cols],
                                  in_=q_grp[:, cols, :].rearrange("p n j -> p (n j)"))
        tile_order = [1, 0, 3, 2]
        for s0 in range(0, N - QUARTER, QUARTER):
            join_keys(s0, s0 + QUARTER, 0, PACK)
        for t0 in (0, 2):
            join_keys(N - QUARTER, N, t0, t0 + 2)

        score_ps = [ps.tile([P, NQ], F32, name=f"score_ps{t}", tag=f"bank{t}") for t in range(PACK)]
        for t in tile_order:
            cols = slice(t * P, (t + 1) * P)
            nc.vector.quantize_mx(out=k_codes[:, cols].bitcast(FP8X4), scales=k_scales[:, cols],
                                  in_=k_grp[:, t * P * PACK:(t + 1) * P * PACK])
        for t in tile_order:
            cols = slice(t * P, (t + 1) * P)
            nc.tensor.matmul_mx(out=score_ps[t][:], lhsT=k_codes[:, cols].bitcast(FP8X4),
                                lhsT_scale=k_scales[:, cols], rhs=q_codes[:].bitcast(FP8X4),
                                rhs_scale=q_scales[:], start=True, stop=True)

        v_ps = [ps.tile([P, 2, P], F32, name="v_ps0", tag="bank1"), ps.tile([P, 2, P], F32, name="v_ps1")]
        v_scales = [sb.tile([P, P], U8, name=f"v_scales{b}", align_bytes=64) for b in range(2)]
        v_codes = [reuse.tile([P, P], U32, name="v_codes0", offset=0, align_bytes=256),
                   reuse.tile([P, P], U32, name="v_codes1", offset=4 * T, align_bytes=256)]
        capped = [sb.tile([P, 2, NQ + 4], F32, name=f"capped{i}", tag=f"capped{i}", align_bytes=64) for i in range(2)]
        v_grp = [sb.tile([P, P * PACK], BF16, name="v_grp0", tag="capped0", align_bytes=64),
                 sb.tile([P, P * PACK], BF16, name="v_grp1", align_bytes=64)]

        def turn_values(b, planes):
            for w in range(2):
                nc.tensor.transpose(v_ps[b][:, w, :], planes[w], ident[:])

        scalar_cast(v_g[0], v_pool[0][:].indirect(offsets[:]))
        words = [v_g[b].bitcast(F32) for b in range(2)]
        turn_values(0, [words[0][:, w:2 * P:2] for w in range(2)])
        nc.vector.tensor_copy(v_g[1].rearrange("p (w m s) -> p m w s", w=2, s=2), v_pool[1][:].indirect(offsets[:]))
        turn_values(1, [words[1][:, w * P:(w + 1) * P] for w in range(2)])

        quarters = [slice(c * NQ // 4, (c + 1) * NQ // 4) for c in range(4)]
        prob = sb.tile([P, 2, NQ + 2, 2], F32, name="prob")
        w_grp = [reuse.tile([P, NQ // 2, PACK], BF16, name=f"w_grp{h}", offset=4 * T + h * NQ * PACK, align_bytes=256)
                 for h in range(2)]
        w_codes = sb.tile([P, NQ], U32, name="w_codes", align_bytes=64)
        w_scales = sb.tile([P, NQ], U8, name="w_scales", align_bytes=64)

        def sigmoid(i, cols):
            nc.scalar.activation(prob[:, i, cols, :], capped[i][:, :, cols].rearrange("p s n -> p n s"),
                                 ACT.Sigmoid, scale=2.0)

        for t in tile_order:
            nc.scalar.activation(capped[t // 2][:, t % 2, 0:NQ], score_ps[t][:], ACT.Tanh, scale=0.5)
        sigmoid(0, slice(0, NQ))
        for cols in quarters:
            sigmoid(1, cols)

        def leave_psum(b, features):
            nc.scalar.copy(v_grp[b][:].bitcast(F32).rearrange("p (e w) -> p e w", w=2)[:, features, :],
                           v_ps[b][:].rearrange("p w e -> p e w")[:, features, :])

        def quantise_values(b, features):
            nc.vector.quantize_mx(out=v_codes[b][:, features].bitcast(FP8X4), scales=v_scales[b][:, features],
                                  in_=v_grp[b][:, features.start * PACK:features.stop * PACK])

        pieces = [(0, slice(0, P)), (1, slice(0, P // 2)), (1, slice(P // 2, P))]
        for b, features in pieces:
            leave_psum(b, features)
        scales = vs_turned.rearrange("p (i s) -> p i s", i=2).unsqueeze(1).to_broadcast([P, NQ // 4, 2, 2])
        for c, cols in enumerate(quarters):
            nc.vector.tensor_tensor(w_grp[c // 2][:, quarters[c % 2], :].rearrange("p n (i s) -> p n i s", i=2),
                                    prob[:, :, cols, :].rearrange("p i n s -> p n i s"), scales, ALU.mult)
        for h, cols in enumerate(query_halves):
            nc.vector.quantize_mx(out=w_codes[:, cols].bitcast(FP8X4), scales=w_scales[:, cols],
                                  in_=w_grp[h][:].rearrange("p n t -> p (n t)"))
        for b, features in pieces:
            quantise_values(b, features)

        y = sb.tile([P, DV], F32, name="y", align_bytes=256)
        for k, (b, features) in enumerate(pieces):
            width = features.stop - features.start
            y_ps = ps.tile([P, width], F32, name=f"y_ps{k}", tag=f"bank{tile_order[k + 1]}")
            nc.tensor.matmul_mx(out=y_ps[:], lhsT=w_codes[:].bitcast(FP8X4), lhsT_scale=w_scales[:],
                                rhs=v_codes[b][:, features].bitcast(FP8X4), rhs_scale=v_scales[b][:, features],
                                start=True, stop=True)
            dst = y[:, b * P + features.start:b * P + features.stop]
            if b == 0:
                nc.vector.tensor_scalar(dst, y_ps[:], 1.0 / 16.0, None, ALU.mult)
            else:
                nc.scalar.activation(dst, y_ps[:], ACT.Copy, scale=1.0 / 16.0)
        nc.sync.dma_start(out[0, :, 0:P], y[:, 0:P])
        nc.scalar.dma_start(out[0, :, P:DV], y[:, P:DV])
